import numpy as np
import ml_dtypes


def mxq(x, axis, fmt="e4m3"):
    dtype, down = {"e4m3": (ml_dtypes.float8_e4m3fn, 7), "e5m2": (ml_dtypes.float8_e5m2, 14)}[fmt]
    v = np.moveaxis(np.asarray(x, np.float32).astype(ml_dtypes.bfloat16).astype(np.float64), axis, -1)
    blocks = v.reshape(v.shape[:-1] + (-1, 32))
    amax = np.abs(blocks).max(-1, keepdims=True)
    byte = np.maximum(np.where(amax > 0, np.frexp(amax)[1] - 1 + 127, 0) - down, 1)
    scale = np.exp2(byte - 127.0)
    codes = (blocks / scale).astype(np.float32).astype(dtype).astype(np.float64)
    return np.moveaxis((codes * scale).reshape(v.shape), -1, axis)


WIDE = False


def mx_kscale(k):
    if not WIDE:
        return np.ones(k)
    levels = np.array([10, -10, 5, -5, 0])
    if k % 512:
        return np.exp2(np.random.permutation(np.resize(levels, k // 32))).repeat(32)
    a = np.empty((k // 512, 16))
    for p in range(k // 512):
        a[p, :8] = np.random.permutation(np.resize(levels, 8))
        for g in range(8):
            far = levels[np.abs(levels - a[p, g]) >= 10]
            a[p, g + 8] = far[np.random.randint(len(far))]
    return np.exp2(a.ravel()).repeat(32)


def f64(x):
    return np.asarray(x).astype(np.float64)


def striped(idx):
    return np.tile(idx.reshape(-1, 16).T, (8, 1)).astype(np.uint16)


def unstriped(offs):
    return offs[:16].T.reshape(-1).astype(np.int64)


E2M1 = np.array([0.0, 0.5, 1.0, 1.5, 2.0, 3.0, 4.0, 6.0, -0.0, -0.5, -1.0, -1.5, -2.0, -3.0, -4.0, -6.0])


def pack_fp4(w):
    k, n = w.shape
    w = f64(np.asarray(w, np.float32).astype(ml_dtypes.bfloat16)).reshape(k // 32, 32, n)
    amax = np.abs(w).max(1)
    mant, ex = np.frexp(amax / 6.0)
    byte = np.clip(np.where(amax > 0, np.where(mant > 0.5, ex, ex - 1) + 127, 1), 1, 254)
    scaled = (w * np.exp2(127.0 - byte)[:, None, :]).reshape(k, n).astype(np.float32)
    c = np.ascontiguousarray(scaled.reshape(k // 512, 128, 4, n).transpose(0, 1, 3, 2)).astype(ml_dtypes.float4_e2m1fn).view(np.uint8) & 0xF
    words = (c[..., 0::2] | (c[..., 1::2] << 4)).reshape(k // 512, 128, 2 * n)
    return np.ascontiguousarray(words), np.ascontiguousarray(byte.astype(np.uint8).reshape(k // 512, 16, n))


def unpack_fp4(words, scales):
    g, _, n = scales.shape
    words = np.ascontiguousarray(words).reshape(g, 128, n, 2)
    nib = np.empty((g, 128, n, 4), np.uint8)
    nib[..., 0::2] = words & 0xF
    nib[..., 1::2] = words >> 4
    vals = E2M1[nib] * np.repeat(np.exp2(scales.astype(np.float64) - 127.0), 8, axis=1)[..., None]
    return vals.transpose(0, 1, 3, 2).reshape(g * 512, n)


K, T, S, H, N = 1024, 1024, 512, 512, 256
P = 2 ** 7


def setup_inputs():
    n = np.random.standard_normal
    s = mx_kscale(K)[:, None]
    u = mx_kscale(H)
    packed_w2 = pack_fp4(n((H, N)) / np.sqrt(H) / u[:, None])
    return {
        "xT": (n((K, T)) * s).astype(np.float32),
        "w1": (n((K, H)) / np.sqrt(K) / s * u).astype(np.float32),
        "w2_words": packed_w2[0],
        "w2_scales": packed_w2[1],
        "lam": np.tile(np.random.uniform(0.1, 0.9, S), (P, 1)).astype(np.float32),
        "mu": np.tile(np.random.uniform(0.1, 0.9, S), (P, 1)).astype(np.float32),
        "offs": striped(np.random.permutation(T)[:S]),
        "pos1": striped(np.random.permutation(S)),
    }


def reference(xT, w1, w2_words, w2_scales, lam, mu, offs, pos1):
    xq = mxq(f64(xT)[:, unstriped(offs)], 0, "e4m3")
    h = mxq(f64(w1), 0, "e4m3").T @ xq
    z = h * f64(lam)[:1] + h[:, unstriped(pos1)] * f64(mu)[:1]
    return unpack_fp4(w2_words, w2_scales).T @ mxq(z, 0, "e4m3")

@@ -1,0 +1,179 @@
+from contextlib import ExitStack
+
+import concourse.mybir as mybir
+
+K, T, S, H, N = 1024, 1024, 512, 512, 256
+FLOPS = 2 * K * H * S + 2 * H * N * S
+
+F32 = mybir.dt.float32
+BF16 = mybir.dt.bfloat16
+I32 = mybir.dt.int32
+U32 = mybir.dt.uint32
+U16 = mybir.dt.uint16
+U8 = mybir.dt.uint8
+FP8X4 = mybir.dt.float8_e4m3fn_x4
+FP4X4 = mybir.dt.float4_e2m1fn_x4
+COPY = mybir.ActivationFunctionType.Copy
+MULT = mybir.AluOpType.mult
+ADD = mybir.AluOpType.add
+
+P = 128
+PACK = 4
+K_PASS = P * PACK
+PASSES = K // K_PASS
+LIST_COLS = 16
+
+X_PIECES = [(0, 0, 512), (0, 512, 1024), (1, 0, 512), (1, 512, 768), (1, 768, 1024)]
+W_COLS = 256
+W_M = W_COLS // PACK
+OUT_CHUNKS = [(0, 128), (128, 256), (256, 384), (384, 512)]
+GATHER = 256
+
+
+def tile_picked_mixup_none_e_kernel(
+    tc, xT, w1, w2_words, w2_scales, lam, mu, offs, pos1, out
+):
+    nc = tc.nc
+    with ExitStack() as ctx:
+        keep = ctx.enter_context(tc.tile_pool(name="keep", bufs=1))
+        psum = ctx.enter_context(tc.psum_pool(name="psum", bufs=1))
+
+        def sbuf(shape, dtype, name):
+            return keep.tile(shape, dtype, name=name, align_bytes=64)
+
+        offs_sb = sbuf([P, S // LIST_COLS], U16, "offs_sb")
+        pos_sb = sbuf([P, S // LIST_COLS], U16, "pos_sb")
+        x_scales = sbuf([P, T], U8, "x_scales")
+        w2_scale_sb = sbuf([P, N], U8, "w2_scale_sb")
+        nc.gpsimd.memset(x_scales[:], 0)
+        nc.gpsimd.memset(w2_scale_sb[:], 0)
+
+        x_raw = []
+        for i, (g, c0, c1) in enumerate(X_PIECES):
+            raw = sbuf([P, PACK, c1 - c0], F32, "x_raw%d" % i)
+            rows = xT[g * K_PASS : (g + 1) * K_PASS, c0:c1]
+            nc.sync.dma_start(out=raw[:], in_=rows.rearrange("(p j) c -> p j c", j=PACK))
+            x_raw.append(raw)
+            if i == 0:
+                nc.sync.dma_start(offs_sb[:], offs)
+        w_raw = {}
+        for g in range(PASSES):
+            for b in range(H // W_COLS):
+                raw = sbuf([P, PACK, W_COLS], F32, "w_raw%d_%d" % (g, b))
+                rows = w1[g * K_PASS : (g + 1) * K_PASS, b * W_COLS : (b + 1) * W_COLS]
+                nc.sync.dma_start(out=raw[:], in_=rows.rearrange("(p j) c -> p j c", j=PACK))
+                w_raw.setdefault((g, b), raw)
+        mu_sb = sbuf([P, S], F32, "mu_sb")
+        lam_sb = sbuf([P, S], F32, "lam_sb")
+        w2_sb = sbuf([P, 2 * N], U8, "w2_sb")
+        nc.sync.dma_start(pos_sb[:], pos1)
+        nc.sync.dma_start(out=mu_sb[:], in_=mu)
+        nc.sync.dma_start(out=lam_sb[:], in_=lam)
+        nc.sync.dma_start(out=w2_sb[:], in_=w2_words[0])
+        for q in range(4):
+            nc.sync.dma_start(
+                out=w2_scale_sb[32 * q : 32 * q + 4, :].bitcast(I32),
+                in_=w2_scales[0, 4 * q : 4 * q + 4, :].bitcast(I32),
+            )
+
+        x_words = [sbuf([P, T], U32, "x_words%d" % g) for g in range(PASSES)]
+        picked_words = [sbuf([P, S], U32, "picked_words%d" % g) for g in range(PASSES)]
+        picked_scales = sbuf([P, S], U8, "picked_scales")
+        for i, (g, c0, c1) in enumerate(X_PIECES):
+            width = c1 - c0
+            grouped = sbuf([P, width, PACK], BF16, "x_grouped%d" % i)
+            cut = width * 5 // 8
+            src = x_raw[i]
+            nc.vector.tensor_copy(
+                out=grouped[:, :cut, :].rearrange("p (c i) j -> p c j i", i=4),
+                in_=src[:, :, :cut].rearrange("p j (c i) -> p c j i", i=4),
+            )
+            nc.scalar.activation(
+                grouped[:, cut:, :].rearrange("p (c i) j -> p c j i", i=4),
+                src[:, :, cut:].rearrange("p j (c i) -> p c j i", i=4),
+                COPY,
+            )
+            nc.vector.quantize_mx(
+                out=x_words[g][:, c0:c1].bitcast(FP8X4),
+                scales=x_scales[4 * g :, c0:c1],
+                in_=grouped[:].rearrange("p c j -> p (c j)"),
+            )
+            if c1 == T:
+                nc.vector.tensor_copy(picked_words[g][:], x_words[g][:].indirect(offs_sb[:]))
+        nc.vector.tensor_copy(picked_scales[:], x_scales[:].indirect(offs_sb[:]))
+
+        w_words = [sbuf([P, PACK, P], U32, "w_words%d" % g) for g in range(PASSES)]
+        w_scales = [sbuf([P, PACK, P], U8, "w_scales%d" % g) for g in range(PASSES)]
+        for g in range(PASSES):
+            for b in range(H // W_COLS):
+                src = w_raw[(g, b)][:].rearrange("p j (m t) -> p m j t", t=PACK)
+                last = g == PASSES - 1 and b == H // W_COLS - 1
+                shares = [(0, 2), (2, 4)] if last else [(0, 4)]
+                for t0, t1 in shares:
+                    dealt = sbuf([P, t1 - t0, W_M, PACK], BF16, "w_dealt%d_%d_%d" % (g, b, t0))
+                    dst = dealt[:].rearrange("p t m j -> p m j t")
+                    if last and t0 == 0:
+                        nc.vector.tensor_copy(out=dst, in_=src[:, :, :, t0:t1])
+                    else:
+                        nc.scalar.activation(dst, src[:, :, :, t0:t1], COPY)
+                    for t in range(t0, t1):
+                        m_cols = slice(b * W_M, (b + 1) * W_M)
+                        nc.vector.quantize_mx(
+                            out=w_words[g][:, t, m_cols].bitcast(FP8X4),
+                            scales=w_scales[g][:, t, m_cols],
+                            in_=dealt[:, t - t0, :, :].rearrange("p m j -> p (m j)"),
+                        )
+
+        own = sbuf([P, PACK, S], F32, "own")
+        partner = sbuf([P, PACK, S], F32, "partner")
+        for t in range(PACK):
+            h_ps = psum.tile([P, S], F32, name="h_ps%d" % t)
+            for g in range(PASSES):
+                nc.tensor.matmul_mx(
+                    out=h_ps[:],
+                    lhsT=w_words[g][:, t, :].bitcast(FP8X4),
+                    lhsT_scale=w_scales[g][:, t, :],
+                    rhs=picked_words[g][:].bitcast(FP8X4),
+                    rhs_scale=picked_scales[4 * g :, :],
+                    start=(g == 0),
+                    stop=(g == PASSES - 1),
+                )
+            h_sb = sbuf([P, S], F32, "h_sb%d" % t)
+            nc.scalar.activation(h_sb[:], h_ps[:], COPY)
+            for c0 in range(0, S, GATHER):
+                cols = slice(c0, c0 + GATHER)
+                places = pos_sb[:, c0 // LIST_COLS : (c0 + GATHER) // LIST_COLS]
+                nc.vector.tensor_tensor(partner[:, t, cols], h_sb[:].indirect(places), mu_sb[:, cols], MULT)
+            nc.vector.tensor_tensor(own[:, t, :], h_sb[:], lam_sb[:], MULT)
+
+        out_view = out.rearrange("(h p) s -> p h s", p=P)
+        for i, (c0, c1) in enumerate(OUT_CHUNKS):
+            width = c1 - c0
+            z_grouped = sbuf([P, width, PACK], BF16, "z_grouped%d" % i)
+            nc.vector.tensor_tensor(
+                z_grouped[:].rearrange("p (c i) t -> p c t i", i=4),
+                own[:, :, c0:c1].rearrange("p t (c i) -> p c t i", i=4),
+                partner[:, :, c0:c1].rearrange("p t (c i) -> p c t i", i=4),
+                ADD,
+            )
+            z_words = sbuf([P, width], U32, "z_words%d" % i)
+            z_scales = sbuf([P, width], U8, "z_scales%d" % i)
+            nc.vector.quantize_mx(
+                out=z_words[:].bitcast(FP8X4),
+                scales=z_scales[:],
+                in_=z_grouped[:].rearrange("p c t -> p (c t)"),
+            )
+            out_ps = psum.tile([P, N // P, width], F32, name="out_ps%d" % i)
+            for h in range(N // P):
+                nc.tensor.matmul_mx(
+                    out=out_ps[:, h, :],
+                    lhsT=w2_sb[:, 2 * P * h : 2 * P * (h + 1)].bitcast(FP4X4),
+                    lhsT_scale=w2_scale_sb[:, P * h : P * (h + 1)],
+                    rhs=z_words[:].bitcast(FP8X4),
+                    rhs_scale=z_scales[:],
+                    start=True,
+                    stop=True,
+                )
+            out_sb = sbuf([P, N // P, width], F32, "out_sb%d" % i)
+            nc.scalar.activation(out_sb[:], out_ps[:], COPY)
+            nc.sync.dma_start(out=out_view[:, :, c0:c1], in_=out_sb[:])

@@ -1,6 +1,7 @@
 from contextlib import ExitStack
 
 import concourse.mybir as mybir
+from concourse.masks import make_identity
 
 K, T, S, H, N = 1024, 1024, 512, 512, 256
 FLOPS = 2 * K * H * S + 2 * H * N * S
@@ -21,13 +22,18 @@ P = 128
 PACK = 4
 K_PASS = P * PACK
 PASSES = K // K_PASS
-LIST_COLS = 16
+QUADRANT = 32
+SCALE_ROWS = 4
+LIST_ROWS = 16
+RUN = 4
 
-X_PIECES = [(0, 0, 512), (0, 512, 1024), (1, 0, 512), (1, 512, 768), (1, 768, 1024)]
-W_COLS = 256
-W_M = W_COLS // PACK
-OUT_CHUNKS = [(0, 128), (128, 256), (256, 384), (384, 512)]
-GATHER = 256
+X_PIECE = 512
+X_VECTOR_SHARE = [352, 336, 192, 336]
+W_VECTOR_SHARE = 72
+GATHER = S // 2
+CHUNK = P
+CHUNKS = S // CHUNK
+DIRECT = 1
 
 
 def tile_picked_mixup_none_e_kernel(
@@ -38,142 +44,161 @@ def tile_picked_mixup_none_e_kernel(
         keep = ctx.enter_context(tc.tile_pool(name="keep", bufs=1))
         psum = ctx.enter_context(tc.psum_pool(name="psum", bufs=1))
 
-        def sbuf(shape, dtype, name):
-            return keep.tile(shape, dtype, name=name, align_bytes=64)
+        def sbuf(shape, dtype, name, tag=""):
+            return keep.tile(shape, dtype, name=name, tag=tag, align_bytes=64)
 
-        offs_sb = sbuf([P, S // LIST_COLS], U16, "offs_sb")
-        pos_sb = sbuf([P, S // LIST_COLS], U16, "pos_sb")
         x_scales = sbuf([P, T], U8, "x_scales")
         w2_scale_sb = sbuf([P, N], U8, "w2_scale_sb")
         nc.gpsimd.memset(x_scales[:], 0)
         nc.gpsimd.memset(w2_scale_sb[:], 0)
+        ident = sbuf([P, P], F32, "ident")
+        make_identity(nc, ident[:])
 
+        offs_sb = sbuf([P, S // LIST_ROWS], U16, "offs_sb")
+        pos_sb = sbuf([P, S // LIST_ROWS], U16, "pos_sb")
+        x_pieces = [(g, c0) for g in range(PASSES) for c0 in range(0, T, X_PIECE)]
         x_raw = []
-        for i, (g, c0, c1) in enumerate(X_PIECES):
-            raw = sbuf([P, PACK, c1 - c0], F32, "x_raw%d" % i)
-            rows = xT[g * K_PASS : (g + 1) * K_PASS, c0:c1]
+        for g, c0 in x_pieces:
+            raw = sbuf([P, PACK, X_PIECE], F32, "x_raw%d_%d" % (g, c0))
+            rows = xT[g * K_PASS : (g + 1) * K_PASS, c0 : c0 + X_PIECE]
             nc.sync.dma_start(out=raw[:], in_=rows.rearrange("(p j) c -> p j c", j=PACK))
             x_raw.append(raw)
-            if i == 0:
+            if (g, c0) == (0, 0):
                 nc.sync.dma_start(offs_sb[:], offs)
-        w_raw = {}
+                nc.sync.dma_start(pos_sb[:], pos1)
+        w_raw = []
         for g in range(PASSES):
-            for b in range(H // W_COLS):
-                raw = sbuf([P, PACK, W_COLS], F32, "w_raw%d_%d" % (g, b))
-                rows = w1[g * K_PASS : (g + 1) * K_PASS, b * W_COLS : (b + 1) * W_COLS]
-                nc.sync.dma_start(out=raw[:], in_=rows.rearrange("(p j) c -> p j c", j=PACK))
-                w_raw.setdefault((g, b), raw)
+            raw = sbuf([P, PACK, H], F32, "w_raw%d" % g)
+            rows = w1[g * K_PASS : (g + 1) * K_PASS, :]
+            nc.sync.dma_start(out=raw[:], in_=rows.rearrange("(p j) c -> p j c", j=PACK))
+            w_raw.append(raw)
         mu_sb = sbuf([P, S], F32, "mu_sb")
-        lam_sb = sbuf([P, S], F32, "lam_sb")
-        w2_sb = sbuf([P, 2 * N], U8, "w2_sb")
-        nc.sync.dma_start(pos_sb[:], pos1)
         nc.sync.dma_start(out=mu_sb[:], in_=mu)
-        nc.sync.dma_start(out=lam_sb[:], in_=lam)
+        lam_rows = sbuf([P, DIRECT * CHUNK], F32, "lam_rows")
+        nc.sync.dma_start(out=lam_rows[:], in_=lam[:, : DIRECT * CHUNK])
+        lam_cols = sbuf([P, CHUNKS - DIRECT], F32, "lam_cols")
+        with nc.allow_non_contiguous_dma(reason="one value a partition"):
+            nc.sync.dma_start(out=lam_cols[:], in_=lam[0, DIRECT * CHUNK :].rearrange("(c p) -> p c", p=P))
+        w2_sb = sbuf([P, 2 * N], U8, "w2_sb")
         nc.sync.dma_start(out=w2_sb[:], in_=w2_words[0])
-        for q in range(4):
+        for q in range(P // QUADRANT):
             nc.sync.dma_start(
-                out=w2_scale_sb[32 * q : 32 * q + 4, :].bitcast(I32),
-                in_=w2_scales[0, 4 * q : 4 * q + 4, :].bitcast(I32),
+                out=w2_scale_sb[QUADRANT * q : QUADRANT * q + SCALE_ROWS, :].bitcast(I32),
+                in_=w2_scales[0, SCALE_ROWS * q : SCALE_ROWS * (q + 1), :].bitcast(I32),
             )
 
         x_words = [sbuf([P, T], U32, "x_words%d" % g) for g in range(PASSES)]
         picked_words = [sbuf([P, S], U32, "picked_words%d" % g) for g in range(PASSES)]
         picked_scales = sbuf([P, S], U8, "picked_scales")
-        for i, (g, c0, c1) in enumerate(X_PIECES):
-            width = c1 - c0
-            grouped = sbuf([P, width, PACK], BF16, "x_grouped%d" % i)
-            cut = width * 5 // 8
-            src = x_raw[i]
+        for (g, c0), raw, cut in zip(x_pieces, x_raw, X_VECTOR_SHARE):
+            grouped = sbuf([P, X_PIECE, PACK], BF16, "x_grouped%d_%d" % (g, c0))
             nc.vector.tensor_copy(
-                out=grouped[:, :cut, :].rearrange("p (c i) j -> p c j i", i=4),
-                in_=src[:, :, :cut].rearrange("p j (c i) -> p c j i", i=4),
+                out=grouped[:, :cut, :].rearrange("p (c r) j -> p c j r", r=RUN),
+                in_=raw[:, :, :cut].rearrange("p j (c r) -> p c j r", r=RUN),
             )
             nc.scalar.activation(
-                grouped[:, cut:, :].rearrange("p (c i) j -> p c j i", i=4),
-                src[:, :, cut:].rearrange("p j (c i) -> p c j i", i=4),
+                grouped[:, cut:, :].rearrange("p (c r) j -> p c j r", r=RUN),
+                raw[:, :, cut:].rearrange("p j (c r) -> p c j r", r=RUN),
                 COPY,
             )
             nc.vector.quantize_mx(
-                out=x_words[g][:, c0:c1].bitcast(FP8X4),
-                scales=x_scales[4 * g :, c0:c1],
+                out=x_words[g][:, c0 : c0 + X_PIECE].bitcast(FP8X4),
+                scales=x_scales[SCALE_ROWS * g :, c0 : c0 + X_PIECE],
                 in_=grouped[:].rearrange("p c j -> p (c j)"),
             )
-            if c1 == T:
+            if c0 + X_PIECE == T:
                 nc.vector.tensor_copy(picked_words[g][:], x_words[g][:].indirect(offs_sb[:]))
         nc.vector.tensor_copy(picked_scales[:], x_scales[:].indirect(offs_sb[:]))
 
-        w_words = [sbuf([P, PACK, P], U32, "w_words%d" % g) for g in range(PASSES)]
-        w_scales = [sbuf([P, PACK, P], U8, "w_scales%d" % g) for g in range(PASSES)]
-        for g in range(PASSES):
-            for b in range(H // W_COLS):
-                src = w_raw[(g, b)][:].rearrange("p j (m t) -> p m j t", t=PACK)
-                last = g == PASSES - 1 and b == H // W_COLS - 1
-                shares = [(0, 2), (2, 4)] if last else [(0, 4)]
-                for t0, t1 in shares:
-                    dealt = sbuf([P, t1 - t0, W_M, PACK], BF16, "w_dealt%d_%d_%d" % (g, b, t0))
-                    dst = dealt[:].rearrange("p t m j -> p m j t")
-                    if last and t0 == 0:
-                        nc.vector.tensor_copy(out=dst, in_=src[:, :, :, t0:t1])
-                    else:
-                        nc.scalar.activation(dst, src[:, :, :, t0:t1], COPY)
-                    for t in range(t0, t1):
-                        m_cols = slice(b * W_M, (b + 1) * W_M)
-                        nc.vector.quantize_mx(
-                            out=w_words[g][:, t, m_cols].bitcast(FP8X4),
-                            scales=w_scales[g][:, t, m_cols],
-                            in_=dealt[:, t - t0, :, :].rearrange("p m j -> p (m j)"),
-                        )
-
-        own = sbuf([P, PACK, S], F32, "own")
-        partner = sbuf([P, PACK, S], F32, "partner")
-        for t in range(PACK):
-            h_ps = psum.tile([P, S], F32, name="h_ps%d" % t)
+        w_words, w_scales = {}, {}
+        for pair in range(PACK // 2):
             for g in range(PASSES):
-                nc.tensor.matmul_mx(
-                    out=h_ps[:],
-                    lhsT=w_words[g][:, t, :].bitcast(FP8X4),
-                    lhsT_scale=w_scales[g][:, t, :],
-                    rhs=picked_words[g][:].bitcast(FP8X4),
-                    rhs_scale=picked_scales[4 * g :, :],
-                    start=(g == 0),
-                    stop=(g == PASSES - 1),
-                )
+                urgent = (pair, g) == (0, PASSES - 1)
+                dealt = sbuf([P, 2, P, PACK], BF16, "w_dealt%d_%d" % (pair, g), "urgent" if urgent else "")
+                src = w_raw[g][:].rearrange("p j (m t) -> p m j t", t=PACK)[:, :, :, 2 * pair : 2 * pair + 2]
+                dst = dealt[:].rearrange("p t m j -> p m j t")
+                cut = W_VECTOR_SHARE if urgent else 0
+                if urgent:
+                    nc.vector.tensor_copy(out=dst[:, :cut], in_=src[:, :cut])
+                nc.scalar.activation(dst[:, cut:], src[:, cut:], COPY)
+                words = sbuf([P, 2 * P], U32, "w_words%d_%d" % (pair, g), "urgent" if (pair, g) == (1, 0) else "")
+                scales = sbuf([P, 2 * P], U8, "w_scales%d_%d" % (pair, g))
+                step = P if urgent else 2 * P
+                flat = dealt[:].rearrange("p t m j -> p (t m j)")
+                for m0 in range(0, 2 * P, step):
+                    nc.vector.quantize_mx(
+                        out=words[:, m0 : m0 + step].bitcast(FP8X4),
+                        scales=scales[:, m0 : m0 + step],
+                        in_=flat[:, PACK * m0 : PACK * (m0 + step)],
+                    )
+                for t in range(2):
+                    w_words.setdefault((g, 2 * pair + t), words[:, t * P : (t + 1) * P])
+                    w_scales.setdefault((g, 2 * pair + t), scales[:, t * P : (t + 1) * P])
+
+        partner = sbuf([P, PACK, S], F32, "partner")
+        own_direct = sbuf([P, PACK, DIRECT * CHUNK], F32, "own_direct")
+        turned = {c: psum.tile([P, PACK, P], F32, name="turned%d" % c, tag="bank_b%d" % c) for c in range(DIRECT, CHUNKS)}
+        for t in range(PACK):
             h_sb = sbuf([P, S], F32, "h_sb%d" % t)
-            nc.scalar.activation(h_sb[:], h_ps[:], COPY)
+            parts = [(0, S // 2, "bank_a0"), (S // 2, S, "bank_a2")] if t == 0 else [(0, S, "bank_a%d" % (t % 2))]
+            for c0, c1, bank in parts:
+                h_ps = psum.tile([P, c1 - c0], F32, name="h_ps%d_%d" % (t, c0), tag=bank)
+                for g in range(PASSES):
+                    nc.tensor.matmul_mx(
+                        out=h_ps[:],
+                        lhsT=w_words[(g, t)].bitcast(FP8X4),
+                        lhsT_scale=w_scales[(g, t)],
+                        rhs=picked_words[g][:, c0:c1].bitcast(FP8X4),
+                        rhs_scale=picked_scales[SCALE_ROWS * g :, c0:c1],
+                        start=(g == 0),
+                        stop=(g == PASSES - 1),
+                    )
+                nc.scalar.activation(h_sb[:, c0:c1], h_ps[:], COPY)
             for c0 in range(0, S, GATHER):
                 cols = slice(c0, c0 + GATHER)
-                places = pos_sb[:, c0 // LIST_COLS : (c0 + GATHER) // LIST_COLS]
+                places = pos_sb[:, c0 // LIST_ROWS : (c0 + GATHER) // LIST_ROWS]
                 nc.vector.tensor_tensor(partner[:, t, cols], h_sb[:].indirect(places), mu_sb[:, cols], MULT)
-            nc.vector.tensor_tensor(own[:, t, :], h_sb[:], lam_sb[:], MULT)
+            nc.vector.tensor_tensor(own_direct[:, t, :], h_sb[:, : DIRECT * CHUNK], lam_rows[:], MULT)
+            for c in range(DIRECT, CHUNKS):
+                nc.tensor.transpose(turned[c][:, t, :], h_sb[:, c * CHUNK : (c + 1) * CHUNK], ident[:])
 
-        out_view = out.rearrange("(h p) s -> p h s", p=P)
-        for i, (c0, c1) in enumerate(OUT_CHUNKS):
-            width = c1 - c0
-            z_grouped = sbuf([P, width, PACK], BF16, "z_grouped%d" % i)
+        own = [own_direct[:, :, c * CHUNK : (c + 1) * CHUNK] for c in range(DIRECT)]
+        for c in range(DIRECT, CHUNKS):
+            scaled = sbuf([P, PACK, P], F32, "scaled%d" % c)
+            nc.scalar.activation(scaled[:], turned[c][:], COPY, scale=lam_cols[:, c - DIRECT : c - DIRECT + 1])
+            back = psum.tile([P, PACK, CHUNK], F32, name="back%d" % c, tag="bank_a%d" % c)
+            for t in range(PACK):
+                nc.tensor.transpose(back[:, t, :], scaled[:, t, :], ident[:])
+            own.append(back[:])
+
+        out_view = out.rearrange("(half p) s -> p half s", p=P)
+        for c in range(CHUNKS):
+            cols = slice(c * CHUNK, (c + 1) * CHUNK)
+            z_grouped = sbuf([P, CHUNK, PACK], BF16, "z_grouped%d" % c)
             nc.vector.tensor_tensor(
-                z_grouped[:].rearrange("p (c i) t -> p c t i", i=4),
-                own[:, :, c0:c1].rearrange("p t (c i) -> p c t i", i=4),
-                partner[:, :, c0:c1].rearrange("p t (c i) -> p c t i", i=4),
+                z_grouped[:].rearrange("p (c r) t -> p c t r", r=RUN),
+                own[c].rearrange("p t (c r) -> p c t r", r=RUN),
+                partner[:, :, cols].rearrange("p t (c r) -> p c t r", r=RUN),
                 ADD,
             )
-            z_words = sbuf([P, width], U32, "z_words%d" % i)
-            z_scales = sbuf([P, width], U8, "z_scales%d" % i)
+            z_words = sbuf([P, CHUNK], U32, "z_words%d" % c)
+            z_scales = sbuf([P, CHUNK], U8, "z_scales%d" % c)
             nc.vector.quantize_mx(
                 out=z_words[:].bitcast(FP8X4),
                 scales=z_scales[:],
                 in_=z_grouped[:].rearrange("p c t -> p (c t)"),
             )
-            out_ps = psum.tile([P, N // P, width], F32, name="out_ps%d" % i)
-            for h in range(N // P):
+            out_sb = sbuf([P, N // P, CHUNK], F32, "out_sb%d" % c)
+            out_ps = psum.tile([P, N // P, CHUNK], F32, name="out_ps%d" % c, tag="bank_b%d" % c)
+            for half in range(N // P):
                 nc.tensor.matmul_mx(
-                    out=out_ps[:, h, :],
-                    lhsT=w2_sb[:, 2 * P * h : 2 * P * (h + 1)].bitcast(FP4X4),
-                    lhsT_scale=w2_scale_sb[:, P * h : P * (h + 1)],
+                    out=out_ps[:, half, :],
+                    lhsT=w2_sb[:, 2 * P * half : 2 * P * (half + 1)].bitcast(FP4X4),
+                    lhsT_scale=w2_scale_sb[:, P * half : P * (half + 1)],
                     rhs=z_words[:].bitcast(FP8X4),
                     rhs_scale=z_scales[:],
                     start=True,
                     stop=True,
                 )
-            out_sb = sbuf([P, N // P, width], F32, "out_sb%d" % i)
             nc.scalar.activation(out_sb[:], out_ps[:], COPY)
-            nc.sync.dma_start(out=out_view[:, :, c0:c1], in_=out_sb[:])
+            nc.sync.dma_start(out=out_view[:, :, cols], in_=out_sb[:])

@@ -28,12 +28,12 @@ LIST_ROWS = 16
 RUN = 4
 
 X_PIECE = 512
-X_VECTOR_SHARE = [352, 336, 192, 336]
-W_VECTOR_SHARE = 72
+X_HALF = X_PIECE // 2
+X_VECTOR_SHARE = [352, 336, 256, 336]
+W_VECTOR_SHARE = 84
 GATHER = S // 2
 CHUNK = P
 CHUNKS = S // CHUNK
-DIRECT = 1
 
 
 def tile_picked_mixup_none_e_kernel(
@@ -74,11 +74,9 @@ def tile_picked_mixup_none_e_kernel(
             w_raw.append(raw)
         mu_sb = sbuf([P, S], F32, "mu_sb")
         nc.sync.dma_start(out=mu_sb[:], in_=mu)
-        lam_rows = sbuf([P, DIRECT * CHUNK], F32, "lam_rows")
-        nc.sync.dma_start(out=lam_rows[:], in_=lam[:, : DIRECT * CHUNK])
-        lam_cols = sbuf([P, CHUNKS - DIRECT], F32, "lam_cols")
+        lam_cols = sbuf([P, CHUNKS], F32, "lam_cols")
         with nc.allow_non_contiguous_dma(reason="one value a partition"):
-            nc.sync.dma_start(out=lam_cols[:], in_=lam[0, DIRECT * CHUNK :].rearrange("(c p) -> p c", p=P))
+            nc.sync.dma_start(out=lam_cols[:], in_=lam[0].rearrange("(c p) -> p c", p=P))
         w2_sb = sbuf([P, 2 * N], U8, "w2_sb")
         nc.sync.dma_start(out=w2_sb[:], in_=w2_words[0])
         for q in range(P // QUADRANT):
@@ -91,21 +89,23 @@ def tile_picked_mixup_none_e_kernel(
         picked_words = [sbuf([P, S], U32, "picked_words%d" % g) for g in range(PASSES)]
         picked_scales = sbuf([P, S], U8, "picked_scales")
         for (g, c0), raw, cut in zip(x_pieces, x_raw, X_VECTOR_SHARE):
-            grouped = sbuf([P, X_PIECE, PACK], BF16, "x_grouped%d_%d" % (g, c0))
-            nc.vector.tensor_copy(
-                out=grouped[:, :cut, :].rearrange("p (c r) j -> p c j r", r=RUN),
-                in_=raw[:, :, :cut].rearrange("p j (c r) -> p c j r", r=RUN),
-            )
-            nc.scalar.activation(
-                grouped[:, cut:, :].rearrange("p (c r) j -> p c j r", r=RUN),
-                raw[:, :, cut:].rearrange("p j (c r) -> p c j r", r=RUN),
-                COPY,
-            )
-            nc.vector.quantize_mx(
-                out=x_words[g][:, c0 : c0 + X_PIECE].bitcast(FP8X4),
-                scales=x_scales[SCALE_ROWS * g :, c0 : c0 + X_PIECE],
-                in_=grouped[:].rearrange("p c j -> p (c j)"),
-            )
+            halves = []
+            for lo in range(0, X_PIECE, X_HALF):
+                grouped = sbuf([P, X_HALF, PACK], BF16, "x_grouped%d_%d" % (g, c0 + lo))
+                dst = grouped[:].rearrange("p (c r) j -> p c j r", r=RUN)
+                src = raw[:, :, lo : lo + X_HALF].rearrange("p j (c r) -> p c j r", r=RUN)
+                runs = min(max(cut - lo, 0), X_HALF) // RUN
+                if runs > 0:
+                    nc.vector.tensor_copy(out=dst[:, :runs], in_=src[:, :runs])
+                if runs < X_HALF // RUN:
+                    nc.scalar.activation(dst[:, runs:], src[:, runs:], COPY)
+                halves.append((c0 + lo, grouped))
+            for lo, grouped in halves:
+                nc.vector.quantize_mx(
+                    out=x_words[g][:, lo : lo + X_HALF].bitcast(FP8X4),
+                    scales=x_scales[SCALE_ROWS * g :, lo : lo + X_HALF],
+                    in_=grouped[:].rearrange("p c j -> p (c j)"),
+                )
             if c0 + X_PIECE == T:
                 nc.vector.tensor_copy(picked_words[g][:], x_words[g][:].indirect(offs_sb[:]))
         nc.vector.tensor_copy(picked_scales[:], x_scales[:].indirect(offs_sb[:]))
@@ -136,11 +136,10 @@ def tile_picked_mixup_none_e_kernel(
                     w_scales.setdefault((g, 2 * pair + t), scales[:, t * P : (t + 1) * P])
 
         partner = sbuf([P, PACK, S], F32, "partner")
-        own_direct = sbuf([P, PACK, DIRECT * CHUNK], F32, "own_direct")
-        turned = {c: psum.tile([P, PACK, P], F32, name="turned%d" % c, tag="bank_b%d" % c) for c in range(DIRECT, CHUNKS)}
+        h_tiles = []
         for t in range(PACK):
             h_sb = sbuf([P, S], F32, "h_sb%d" % t)
-            parts = [(0, S // 2, "bank_a0"), (S // 2, S, "bank_a2")] if t == 0 else [(0, S, "bank_a%d" % (t % 2))]
+            parts = [(0, S // 2, "bank_a0"), (S // 2, S, "bank_b0")] if t == 0 else [(0, S, "bank_a%d" % t)]
             for c0, c1, bank in parts:
                 h_ps = psum.tile([P, c1 - c0], F32, name="h_ps%d_%d" % (t, c0), tag=bank)
                 for g in range(PASSES):
@@ -158,14 +157,16 @@ def tile_picked_mixup_none_e_kernel(
                 cols = slice(c0, c0 + GATHER)
                 places = pos_sb[:, c0 // LIST_ROWS : (c0 + GATHER) // LIST_ROWS]
                 nc.vector.tensor_tensor(partner[:, t, cols], h_sb[:].indirect(places), mu_sb[:, cols], MULT)
-            nc.vector.tensor_tensor(own_direct[:, t, :], h_sb[:, : DIRECT * CHUNK], lam_rows[:], MULT)
-            for c in range(DIRECT, CHUNKS):
+            h_tiles.append(h_sb)
+        turned = {c: psum.tile([P, PACK, P], F32, name="turned%d" % c, tag="bank_b%d" % c) for c in range(CHUNKS)}
+        for t, h_sb in enumerate(h_tiles):
+            for c in range(CHUNKS):
                 nc.tensor.transpose(turned[c][:, t, :], h_sb[:, c * CHUNK : (c + 1) * CHUNK], ident[:])
 
-        own = [own_direct[:, :, c * CHUNK : (c + 1) * CHUNK] for c in range(DIRECT)]
-        for c in range(DIRECT, CHUNKS):
+        own = []
+        for c in range(CHUNKS):
             scaled = sbuf([P, PACK, P], F32, "scaled%d" % c)
-            nc.scalar.activation(scaled[:], turned[c][:], COPY, scale=lam_cols[:, c - DIRECT : c - DIRECT + 1])
+            nc.scalar.activation(scaled[:], turned[c][:], COPY, scale=lam_cols[:, c : c + 1])
             back = psum.tile([P, PACK, CHUNK], F32, name="back%d" % c, tag="bank_a%d" % c)
             for t in range(PACK):
                 nc.tensor.transpose(back[:, t, :], scaled[:, t, :], ident[:])

@@ -107,8 +107,21 @@ def tile_picked_mixup_none_e_kernel(
                     in_=grouped[:].rearrange("p c j -> p (c j)"),
                 )
             if c0 + X_PIECE == T:
+                if g == PASSES - 1:
+                    nc.vector.tensor_copy(picked_scales[:], x_scales[:].indirect(offs_sb[:]))
                 nc.vector.tensor_copy(picked_words[g][:], x_words[g][:].indirect(offs_sb[:]))
-        nc.vector.tensor_copy(picked_scales[:], x_scales[:].indirect(offs_sb[:]))
+
+        warm = psum.tile([P, S], F32, name="warm", tag="bank_b1")
+        for step in range(2):
+            nc.tensor.matmul_mx(
+                out=warm[:],
+                lhsT=picked_words[0][:, :P].bitcast(FP8X4),
+                lhsT_scale=picked_scales[:, :P],
+                rhs=picked_words[0][:].bitcast(FP8X4),
+                rhs_scale=picked_scales[:],
+                start=True,
+                stop=True,
+            )
 
         w_words, w_scales = {}, {}
         for pair in range(PACK // 2):

@@ -29,8 +29,8 @@ RUN = 4
 
 X_PIECE = 512
 X_HALF = X_PIECE // 2
-X_VECTOR_SHARE = [352, 336, 256, 336]
-W_VECTOR_SHARE = 84
+X_VECTOR_SHARE = [352, 320, 208, 304]
+W_VECTOR_SHARE = 76
 GATHER = S // 2
 CHUNK = P
 CHUNKS = S // CHUNK
@@ -203,16 +203,23 @@ def tile_picked_mixup_none_e_kernel(
                 in_=z_grouped[:].rearrange("p c t -> p (c t)"),
             )
             out_sb = sbuf([P, N // P, CHUNK], F32, "out_sb%d" % c)
-            out_ps = psum.tile([P, N // P, CHUNK], F32, name="out_ps%d" % c, tag="bank_b%d" % c)
-            for half in range(N // P):
-                nc.tensor.matmul_mx(
-                    out=out_ps[:, half, :],
-                    lhsT=w2_sb[:, 2 * P * half : 2 * P * (half + 1)].bitcast(FP4X4),
-                    lhsT_scale=w2_scale_sb[:, P * half : P * (half + 1)],
-                    rhs=z_words[:].bitcast(FP8X4),
-                    rhs_scale=z_scales[:],
-                    start=True,
-                    stop=True,
-                )
-            nc.scalar.activation(out_sb[:], out_ps[:], COPY)
+            parts = [[0], [1]] if c == CHUNKS - 1 else [[0, 1]]
+            for halves in parts:
+                first = halves[0]
+                bank = "bank_a0" if first > 0 else "bank_b%d" % c
+                out_ps = psum.tile([P, len(halves), CHUNK], F32, name="out_ps%d_%d" % (c, first), tag=bank)
+                for half in halves:
+                    nc.tensor.matmul_mx(
+                        out=out_ps[:, half - first, :],
+                        lhsT=w2_sb[:, 2 * P * half : 2 * P * (half + 1)].bitcast(FP4X4),
+                        lhsT_scale=w2_scale_sb[:, P * half : P * (half + 1)],
+                        rhs=z_words[:].bitcast(FP8X4),
+                        rhs_scale=z_scales[:],
+                        start=True,
+                        stop=True,
+                    )
+                if first > 0:
+                    nc.vector.tensor_copy(out_sb[:, first:, :], out_ps[:])
+                else:
+                    nc.scalar.activation(out_sb[:, : len(halves), :], out_ps[:], COPY)
             nc.sync.dma_start(out=out_view[:, :, cols], in_=out_sb[:])

@@ -65,13 +65,13 @@ def tile_picked_mixup_none_e_kernel(
             x_raw.append(raw)
             if (g, c0) == (0, 0):
                 nc.sync.dma_start(offs_sb[:], offs)
-                nc.sync.dma_start(pos_sb[:], pos1)
         w_raw = []
         for g in range(PASSES):
             raw = sbuf([P, PACK, H], F32, "w_raw%d" % g)
             rows = w1[g * K_PASS : (g + 1) * K_PASS, :]
             nc.sync.dma_start(out=raw[:], in_=rows.rearrange("(p j) c -> p j c", j=PACK))
             w_raw.append(raw)
+        nc.sync.dma_start(pos_sb[:], pos1)
         mu_sb = sbuf([P, S], F32, "mu_sb")
         nc.sync.dma_start(out=mu_sb[:], in_=mu)
         lam_cols = sbuf([P, CHUNKS], F32, "lam_cols")
@@ -111,7 +111,7 @@ def tile_picked_mixup_none_e_kernel(
                     nc.vector.tensor_copy(picked_scales[:], x_scales[:].indirect(offs_sb[:]))
                 nc.vector.tensor_copy(picked_words[g][:], x_words[g][:].indirect(offs_sb[:]))
 
-        warm = psum.tile([P, S], F32, name="warm", tag="bank_b1")
+        warm = psum.tile([P, S], F32, name="warm", tag="bank_a1")
         for step in range(2):
             nc.tensor.matmul_mx(
                 out=warm[:],
@@ -152,7 +152,7 @@ def tile_picked_mixup_none_e_kernel(
         h_tiles = []
         for t in range(PACK):
             h_sb = sbuf([P, S], F32, "h_sb%d" % t)
-            parts = [(0, S // 2, "bank_a0"), (S // 2, S, "bank_b0")] if t == 0 else [(0, S, "bank_a%d" % t)]
+            parts = [(0, S // 2, "bank_a0"), (S // 2, S, "bank_b0")] if t == 0 else [(0, S, "bank_b%d" % t)]
             for c0, c1, bank in parts:
                 h_ps = psum.tile([P, c1 - c0], F32, name="h_ps%d_%d" % (t, c0), tag=bank)
                 for g in range(PASSES):
@@ -172,13 +172,13 @@ def tile_picked_mixup_none_e_kernel(
                 nc.vector.tensor_tensor(partner[:, t, cols], h_sb[:].indirect(places), mu_sb[:, cols], MULT)
             h_tiles.append(h_sb)
         turned = {c: psum.tile([P, PACK, P], F32, name="turned%d" % c, tag="bank_b%d" % c) for c in range(CHUNKS)}
-        for t, h_sb in enumerate(h_tiles):
-            for c in range(CHUNKS):
+        for c in range(CHUNKS):
+            for t, h_sb in enumerate(h_tiles):
                 nc.tensor.transpose(turned[c][:, t, :], h_sb[:, c * CHUNK : (c + 1) * CHUNK], ident[:])
 
         own = []
         for c in range(CHUNKS):
-            scaled = sbuf([P, PACK, P], F32, "scaled%d" % c)
+            scaled = sbuf([P, PACK, P], F32, "scaled%d" % c, "scaled%d" % c)
             nc.scalar.activation(scaled[:], turned[c][:], COPY, scale=lam_cols[:, c : c + 1])
             back = psum.tile([P, PACK, CHUNK], F32, name="back%d" % c, tag="bank_a%d" % c)
             for t in range(PACK):
@@ -195,7 +195,7 @@ def tile_picked_mixup_none_e_kernel(
                 partner[:, :, cols].rearrange("p t (c r) -> p c t r", r=RUN),
                 ADD,
             )
-            z_words = sbuf([P, CHUNK], U32, "z_words%d" % c)
+            z_words = sbuf([P, CHUNK], U32, "z_words%d" % c, "scaled%d" % (c + 2) if c + 2 < CHUNKS else "")
             z_scales = sbuf([P, CHUNK], U8, "z_scales%d" % c)
             nc.vector.quantize_mx(
                 out=z_words[:].bitcast(FP8X4),

@@ -27,13 +27,13 @@ SCALE_ROWS = 4
 LIST_ROWS = 16
 RUN = 4
 
-X_PIECE = 512
-X_HALF = X_PIECE // 2
-X_VECTOR_SHARE = [352, 320, 208, 304]
-W_VECTOR_SHARE = 76
 GATHER = S // 2
 CHUNK = P
 CHUNKS = S // CHUNK
+HALF = S // 2
+X_WEAVE_VECTOR = 344
+W_FIRST_VECTOR = 32
+SCALAR_TILE = PACK - 1
 
 
 def tile_picked_mixup_none_e_kernel(
@@ -47,30 +47,35 @@ def tile_picked_mixup_none_e_kernel(
         def sbuf(shape, dtype, name, tag=""):
             return keep.tile(shape, dtype, name=name, tag=tag, align_bytes=64)
 
-        x_scales = sbuf([P, T], U8, "x_scales")
+        def entries(offsets, lo, hi):
+            return offsets[:, lo // LIST_ROWS : hi // LIST_ROWS]
+
         w2_scale_sb = sbuf([P, N], U8, "w2_scale_sb")
-        nc.gpsimd.memset(x_scales[:], 0)
         nc.gpsimd.memset(w2_scale_sb[:], 0)
         ident = sbuf([P, P], F32, "ident")
-        make_identity(nc, ident[:])
+        zeros = sbuf([P, P], F32, "zeros")
+        nc.vector.memset(zeros[:], 0.0)
+        nc.scalar.activation(ident[:], zeros[:], COPY)
+        make_identity(nc, ident[:], nomemset=True)
 
         offs_sb = sbuf([P, S // LIST_ROWS], U16, "offs_sb")
         pos_sb = sbuf([P, S // LIST_ROWS], U16, "pos_sb")
-        x_pieces = [(g, c0) for g in range(PASSES) for c0 in range(0, T, X_PIECE)]
-        x_raw = []
-        for g, c0 in x_pieces:
-            raw = sbuf([P, PACK, X_PIECE], F32, "x_raw%d_%d" % (g, c0))
-            rows = xT[g * K_PASS : (g + 1) * K_PASS, c0 : c0 + X_PIECE]
-            nc.sync.dma_start(out=raw[:], in_=rows.rearrange("(p j) c -> p j c", j=PACK))
-            x_raw.append(raw)
-            if (g, c0) == (0, 0):
-                nc.sync.dma_start(offs_sb[:], offs)
-        w_raw = []
+        w_rows = w1.rearrange("(g p j) c -> g p j c", g=PASSES, j=PACK)
+        x_rows = xT.rearrange("(g p j) c -> g p j c", g=PASSES, j=PACK)
+        w_first = sbuf([P, PACK, H], F32, "w_first")
+        x_raw = {}
         for g in range(PASSES):
-            raw = sbuf([P, PACK, H], F32, "w_raw%d" % g)
-            rows = w1[g * K_PASS : (g + 1) * K_PASS, :]
-            nc.sync.dma_start(out=raw[:], in_=rows.rearrange("(p j) c -> p j c", j=PACK))
-            w_raw.append(raw)
+            for j in range(PACK):
+                x_raw[(g, j)] = sbuf([P, T], F32, "x_raw%d_%d" % (g, j))
+                nc.sync.dma_start(out=x_raw[(g, j)][:], in_=x_rows[g, :, j, :])
+                if (g, j) == (0, 0):
+                    nc.sync.dma_start(offs_sb[:], offs)
+        nc.sync.dma_start(out=w_first[:], in_=w_rows[0])
+        w_last = []
+        for u in range(2):
+            raw = sbuf([P, 2, H], F32, "w_last%d" % u)
+            nc.sync.dma_start(out=raw[:], in_=w_rows[1, :, 2 * u : 2 * u + 2, :])
+            w_last.append(raw)
         nc.sync.dma_start(pos_sb[:], pos1)
         mu_sb = sbuf([P, S], F32, "mu_sb")
         nc.sync.dma_start(out=mu_sb[:], in_=mu)
@@ -85,102 +90,121 @@ def tile_picked_mixup_none_e_kernel(
                 in_=w2_scales[0, SCALE_ROWS * q : SCALE_ROWS * (q + 1), :].bitcast(I32),
             )
 
-        x_words = [sbuf([P, T], U32, "x_words%d" % g) for g in range(PASSES)]
-        picked_words = [sbuf([P, S], U32, "picked_words%d" % g) for g in range(PASSES)]
-        picked_scales = sbuf([P, S], U8, "picked_scales")
-        for (g, c0), raw, cut in zip(x_pieces, x_raw, X_VECTOR_SHARE):
-            halves = []
-            for lo in range(0, X_PIECE, X_HALF):
-                grouped = sbuf([P, X_HALF, PACK], BF16, "x_grouped%d_%d" % (g, c0 + lo))
-                dst = grouped[:].rearrange("p (c r) j -> p c j r", r=RUN)
-                src = raw[:, :, lo : lo + X_HALF].rearrange("p j (c r) -> p c j r", r=RUN)
-                runs = min(max(cut - lo, 0), X_HALF) // RUN
-                if runs > 0:
-                    nc.vector.tensor_copy(out=dst[:, :runs], in_=src[:, :runs])
-                if runs < X_HALF // RUN:
-                    nc.scalar.activation(dst[:, runs:], src[:, runs:], COPY)
-                halves.append((c0 + lo, grouped))
-            for lo, grouped in halves:
-                nc.vector.quantize_mx(
-                    out=x_words[g][:, lo : lo + X_HALF].bitcast(FP8X4),
-                    scales=x_scales[SCALE_ROWS * g :, lo : lo + X_HALF],
-                    in_=grouped[:].rearrange("p c j -> p (c j)"),
-                )
-            if c0 + X_PIECE == T:
-                if g == PASSES - 1:
-                    nc.vector.tensor_copy(picked_scales[:], x_scales[:].indirect(offs_sb[:]))
-                nc.vector.tensor_copy(picked_words[g][:], x_words[g][:].indirect(offs_sb[:]))
+        def quantise(words, scales, grouped):
+            nc.vector.quantize_mx(out=words.bitcast(FP8X4), scales=scales, in_=grouped)
 
-        warm = psum.tile([P, S], F32, name="warm", tag="bank_a1")
-        for step in range(2):
-            nc.tensor.matmul_mx(
-                out=warm[:],
-                lhsT=picked_words[0][:, :P].bitcast(FP8X4),
-                lhsT_scale=picked_scales[:, :P],
-                rhs=picked_words[0][:].bitcast(FP8X4),
-                rhs_scale=picked_scales[:],
-                start=True,
-                stop=True,
-            )
+        x_words = [sbuf([P, S], U32, "x_words%d" % g) for g in range(PASSES)]
+        x_scales = [sbuf([P, S], U8, "x_scales%d" % g) for g in range(PASSES)]
+        for g in range(PASSES):
+            grouped = [sbuf([P, HALF, PACK], BF16, "x_grouped%d_%d" % (g, h)) for h in range(2)]
+            if g == 0:
+                planes = sbuf([P, PACK, S], BF16, "planes")
+            for u in range(2):
+                if g == 0:
+                    picked = planes[:, 2 * u : 2 * u + 2, :]
+                else:
+                    picked = sbuf([P, 2, S], BF16, "picked%d_%d" % (g, u))
+                for e in range(2):
+                    raw = x_raw[(g, 2 * u + e)]
+                    cut = 0 if e == 0 else HALF
+                    if cut > 0:
+                        nc.vector.tensor_copy(picked[:, e, :cut], raw[:].indirect(entries(offs_sb, 0, cut)))
+                    if cut < S:
+                        nc.scalar.activation(picked[:, e, cut:], raw[:].indirect(entries(offs_sb, cut, S)), COPY)
+                if g == 0:
+                    continue
+                cut = S if u == 0 else X_WEAVE_VECTOR
+                for h in range(2):
+                    lo = h * HALF
+                    dst = grouped[h][:, :, 2 * u : 2 * u + 2].rearrange("p (c r) e -> p c e r", r=RUN)
+                    src = picked[:, :, lo : lo + HALF].rearrange("p e (c r) -> p c e r", r=RUN)
+                    runs = min(max(cut - lo, 0), HALF) // RUN
+                    if runs > 0:
+                        nc.vector.tensor_copy(out=dst[:, :runs], in_=src[:, :runs])
+                    if runs < HALF // RUN:
+                        nc.scalar.activation(dst[:, runs:], src[:, runs:], COPY)
+            if g == 0:
+                for h in range(2):
+                    dst = grouped[h][:].rearrange("p (c r) j -> p c j r", r=RUN)
+                    src = planes[:, :, h * HALF : (h + 1) * HALF].rearrange("p j (c r) -> p c j r", r=RUN)
+                    nc.vector.tensor_copy(out=dst, in_=src)
+            for h in range(2):
+                cols = slice(h * HALF, (h + 1) * HALF)
+                quantise(x_words[g][:, cols], x_scales[g][:, cols], grouped[h][:].rearrange("p c j -> p (c j)"))
 
-        w_words, w_scales = {}, {}
-        for pair in range(PACK // 2):
-            for g in range(PASSES):
-                urgent = (pair, g) == (0, PASSES - 1)
-                dealt = sbuf([P, 2, P, PACK], BF16, "w_dealt%d_%d" % (pair, g), "urgent" if urgent else "")
-                src = w_raw[g][:].rearrange("p j (m t) -> p m j t", t=PACK)[:, :, :, 2 * pair : 2 * pair + 2]
-                dst = dealt[:].rearrange("p t m j -> p m j t")
-                cut = W_VECTOR_SHARE if urgent else 0
-                if urgent:
-                    nc.vector.tensor_copy(out=dst[:, :cut], in_=src[:, :cut])
+        w_words = [sbuf([P, H], U32, "w_words%d" % g) for g in range(PASSES)]
+        w_scales = [sbuf([P, H], U8, "w_scales%d" % g) for g in range(PASSES)]
+        for pair in range(2):
+            dealt = sbuf([P, 2, P, PACK], BF16, "w_dealt0_%d" % pair)
+            src = w_first[:].rearrange("p j (m t) -> p m j t", t=PACK)[:, :, :, 2 * pair : 2 * pair + 2]
+            dst = dealt[:].rearrange("p t m j -> p m j t")
+            cut = P if pair == 0 else 24
+            nc.vector.tensor_copy(out=dst[:, :cut], in_=src[:, :cut])
+            if cut < P:
                 nc.scalar.activation(dst[:, cut:], src[:, cut:], COPY)
-                words = sbuf([P, 2 * P], U32, "w_words%d_%d" % (pair, g), "urgent" if (pair, g) == (1, 0) else "")
-                scales = sbuf([P, 2 * P], U8, "w_scales%d_%d" % (pair, g))
-                step = P if urgent else 2 * P
-                flat = dealt[:].rearrange("p t m j -> p (t m j)")
-                for m0 in range(0, 2 * P, step):
-                    nc.vector.quantize_mx(
-                        out=words[:, m0 : m0 + step].bitcast(FP8X4),
-                        scales=scales[:, m0 : m0 + step],
-                        in_=flat[:, PACK * m0 : PACK * (m0 + step)],
-                    )
-                for t in range(2):
-                    w_words.setdefault((g, 2 * pair + t), words[:, t * P : (t + 1) * P])
-                    w_scales.setdefault((g, 2 * pair + t), scales[:, t * P : (t + 1) * P])
+            cols = slice(2 * P * pair, 2 * P * (pair + 1))
+            quantise(w_words[0][:, cols], w_scales[0][:, cols], dealt[:].rearrange("p t m j -> p (t m j)"))
+
+        dealt = [sbuf([P, 2, P, PACK], BF16, "w_dealt1_%d" % pair) for pair in range(2)]
+        for u in range(2):
+            for pair in range(2):
+                src = w_last[u][:].rearrange("p e (m t) -> p m e t", t=PACK)[:, :, :, 2 * pair : 2 * pair + 2]
+                dst = dealt[pair][:, :, :, 2 * u : 2 * u + 2].rearrange("p t m e -> p m e t")
+                if u == 0:
+                    cut = P if pair == 0 else 0
+                else:
+                    cut = 84 if pair == 0 else W_FIRST_VECTOR
+                if cut > 0:
+                    nc.vector.tensor_copy(out=dst[:, :cut], in_=src[:, :cut])
+                if cut < P:
+                    nc.scalar.activation(dst[:, cut:], src[:, cut:], COPY)
+        for t0, t1 in ((0, 1), (1, 2), (2, 4)):
+            cols = slice(t0 * P, t1 * P)
+            flat = dealt[t0 // 2][:].rearrange("p t m j -> p (t m j)")
+            quantise(w_words[1][:, cols], w_scales[1][:, cols], flat[:, t0 % 2 * K_PASS : (t0 % 2 + t1 - t0) * K_PASS])
 
         partner = sbuf([P, PACK, S], F32, "partner")
         h_tiles = []
         for t in range(PACK):
             h_sb = sbuf([P, S], F32, "h_sb%d" % t)
-            parts = [(0, S // 2, "bank_a0"), (S // 2, S, "bank_b0")] if t == 0 else [(0, S, "bank_b%d" % t)]
+            parts = [(0, HALF, "bank0"), (HALF, S, "bank1")] if t == 0 else [(0, S, ["", "bank2", "bank0", "bank1"][t])]
             for c0, c1, bank in parts:
                 h_ps = psum.tile([P, c1 - c0], F32, name="h_ps%d_%d" % (t, c0), tag=bank)
                 for g in range(PASSES):
                     nc.tensor.matmul_mx(
                         out=h_ps[:],
-                        lhsT=w_words[(g, t)].bitcast(FP8X4),
-                        lhsT_scale=w_scales[(g, t)],
-                        rhs=picked_words[g][:, c0:c1].bitcast(FP8X4),
-                        rhs_scale=picked_scales[SCALE_ROWS * g :, c0:c1],
+                        lhsT=w_words[g][:, t * P : (t + 1) * P].bitcast(FP8X4),
+                        lhsT_scale=w_scales[g][:, t * P : (t + 1) * P],
+                        rhs=x_words[g][:, c0:c1].bitcast(FP8X4),
+                        rhs_scale=x_scales[g][:, c0:c1],
                         start=(g == 0),
                         stop=(g == PASSES - 1),
                     )
-                nc.scalar.activation(h_sb[:, c0:c1], h_ps[:], COPY)
+                if (t, c0) == (0, HALF):
+                    nc.vector.tensor_copy(h_sb[:, c0:c1], h_ps[:])
+                else:
+                    nc.scalar.activation(h_sb[:, c0:c1], h_ps[:], COPY)
+            if t == SCALAR_TILE:
+                fetched = sbuf([P, S], F32, "fetched")
             for c0 in range(0, S, GATHER):
                 cols = slice(c0, c0 + GATHER)
-                places = pos_sb[:, c0 // LIST_ROWS : (c0 + GATHER) // LIST_ROWS]
-                nc.vector.tensor_tensor(partner[:, t, cols], h_sb[:].indirect(places), mu_sb[:, cols], MULT)
+                looked_up = h_sb[:].indirect(entries(pos_sb, c0, c0 + GATHER))
+                if t == SCALAR_TILE:
+                    nc.scalar.activation(fetched[:, cols], looked_up, COPY)
+                    nc.vector.tensor_tensor(partner[:, t, cols], fetched[:, cols], mu_sb[:, cols], MULT)
+                else:
+                    nc.vector.tensor_tensor(partner[:, t, cols], looked_up, mu_sb[:, cols], MULT)
             h_tiles.append(h_sb)
-        turned = {c: psum.tile([P, PACK, P], F32, name="turned%d" % c, tag="bank_b%d" % c) for c in range(CHUNKS)}
-        for c in range(CHUNKS):
-            for t, h_sb in enumerate(h_tiles):
+        turned = {c: psum.tile([P, PACK, P], F32, name="turned%d" % c, tag="bank%d" % (4 + c)) for c in range(CHUNKS)}
+        for t, h_sb in enumerate(h_tiles):
+            for c in range(CHUNKS):
                 nc.tensor.transpose(turned[c][:, t, :], h_sb[:, c * CHUNK : (c + 1) * CHUNK], ident[:])
 
         own = []
         for c in range(CHUNKS):
             scaled = sbuf([P, PACK, P], F32, "scaled%d" % c, "scaled%d" % c)
             nc.scalar.activation(scaled[:], turned[c][:], COPY, scale=lam_cols[:, c : c + 1])
-            back = psum.tile([P, PACK, CHUNK], F32, name="back%d" % c, tag="bank_a%d" % c)
+            back = psum.tile([P, PACK, CHUNK], F32, name="back%d" % c, tag="bank%d" % [3, 2, 0, 1][c])
             for t in range(PACK):
                 nc.tensor.transpose(back[:, t, :], scaled[:, t, :], ident[:])
             own.append(back[:])
@@ -206,7 +230,7 @@ def tile_picked_mixup_none_e_kernel(
             parts = [[0], [1]] if c == CHUNKS - 1 else [[0, 1]]
             for halves in parts:
                 first = halves[0]
-                bank = "bank_a0" if first > 0 else "bank_b%d" % c
+                bank = "bank3" if first > 0 else "bank%d" % (4 + c)
                 out_ps = psum.tile([P, len(halves), CHUNK], F32, name="out_ps%d_%d" % (c, first), tag=bank)
                 for half in halves:
                     nc.tensor.matmul_mx(

@@ -132,6 +132,18 @@ def tile_picked_mixup_none_e_kernel(
                 cols = slice(h * HALF, (h + 1) * HALF)
                 quantise(x_words[g][:, cols], x_scales[g][:, cols], grouped[h][:].rearrange("p c j -> p (c j)"))
 
+        warm = psum.tile([P, S], F32, name="warm", tag="bank3")
+        for step in range(2):
+            nc.tensor.matmul_mx(
+                out=warm[:],
+                lhsT=x_words[1][:, :P].bitcast(FP8X4),
+                lhsT_scale=x_scales[1][:, :P],
+                rhs=x_words[1][:].bitcast(FP8X4),
+                rhs_scale=x_scales[1][:],
+                start=True,
+                stop=True,
+            )
+
         w_words = [sbuf([P, H], U32, "w_words%d" % g) for g in range(PASSES)]
         w_scales = [sbuf([P, H], U8, "w_scales%d" % g) for g in range(PASSES)]
         for pair in range(2):

@@ -132,18 +132,6 @@ def tile_picked_mixup_none_e_kernel(
                 cols = slice(h * HALF, (h + 1) * HALF)
                 quantise(x_words[g][:, cols], x_scales[g][:, cols], grouped[h][:].rearrange("p c j -> p (c j)"))
 
-        warm = psum.tile([P, S], F32, name="warm", tag="bank3")
-        for step in range(2):
-            nc.tensor.matmul_mx(
-                out=warm[:],
-                lhsT=x_words[1][:, :P].bitcast(FP8X4),
-                lhsT_scale=x_scales[1][:, :P],
-                rhs=x_words[1][:].bitcast(FP8X4),
-                rhs_scale=x_scales[1][:],
-                start=True,
-                stop=True,
-            )
-
         w_words = [sbuf([P, H], U32, "w_words%d" % g) for g in range(PASSES)]
         w_scales = [sbuf([P, H], U8, "w_scales%d" % g) for g in range(PASSES)]
         for pair in range(2):
@@ -158,18 +146,23 @@ def tile_picked_mixup_none_e_kernel(
             quantise(w_words[0][:, cols], w_scales[0][:, cols], dealt[:].rearrange("p t m j -> p (t m j)"))
 
         dealt = [sbuf([P, 2, P, PACK], BF16, "w_dealt1_%d" % pair) for pair in range(2)]
-        for u in range(2):
-            for pair in range(2):
-                src = w_last[u][:].rearrange("p e (m t) -> p m e t", t=PACK)[:, :, :, 2 * pair : 2 * pair + 2]
-                dst = dealt[pair][:, :, :, 2 * u : 2 * u + 2].rearrange("p t m e -> p m e t")
-                if u == 0:
-                    cut = P if pair == 0 else 0
-                else:
-                    cut = 84 if pair == 0 else W_FIRST_VECTOR
-                if cut > 0:
-                    nc.vector.tensor_copy(out=dst[:, :cut], in_=src[:, :cut])
-                if cut < P:
-                    nc.scalar.activation(dst[:, cut:], src[:, cut:], COPY)
+        def deal(engine, u, tiles, cols):
+            pair = tiles.start // 2
+            src = w_last[u][:].rearrange("p e (m t) -> p m e t", t=PACK)[:, cols, :, tiles]
+            dst = dealt[pair][:, tiles.start % 2 : (tiles.stop - 1) % 2 + 1, cols, 2 * u : 2 * u + 2]
+            dst = dst.rearrange("p t m e -> p m e t")
+            if engine == "vector":
+                nc.vector.tensor_copy(out=dst, in_=src)
+            else:
+                nc.scalar.activation(dst, src, COPY)
+
+        deal("vector", 0, slice(0, 2), slice(0, P))
+        deal("scalar", 0, slice(2, 4), slice(0, P))
+        deal("vector", 1, slice(0, 1), slice(0, 72))
+        deal("scalar", 1, slice(0, 1), slice(72, P))
+        deal("vector", 1, slice(2, 4), slice(0, 48))
+        deal("scalar", 1, slice(1, 2), slice(0, P))
+        deal("scalar", 1, slice(2, 4), slice(48, P))
         for t0, t1 in ((0, 1), (1, 2), (2, 4)):
             cols = slice(t0 * P, t1 * P)
             flat = dealt[t0 // 2][:].rearrange("p t m j -> p (t m j)")
@@ -207,16 +200,28 @@ def tile_picked_mixup_none_e_kernel(
                 else:
                     nc.vector.tensor_tensor(partner[:, t, cols], looked_up, mu_sb[:, cols], MULT)
             h_tiles.append(h_sb)
-        turned = {c: psum.tile([P, PACK, P], F32, name="turned%d" % c, tag="bank%d" % (4 + c)) for c in range(CHUNKS)}
+        turned = {c: psum.tile([P, PACK, P], F32, name="turned%d" % c, tag="bank%d" % (4 + c)) for c in range(CHUNKS - 1)}
         for t, h_sb in enumerate(h_tiles):
-            for c in range(CHUNKS):
+            for c in range(CHUNKS - 1):
                 nc.tensor.transpose(turned[c][:, t, :], h_sb[:, c * CHUNK : (c + 1) * CHUNK], ident[:])
+        last = CHUNKS - 1
+        turned[last] = psum.tile([P, PACK, P], F32, name="turned_last", tag="bank1")
+        for g in range(PASSES):
+            nc.tensor.matmul_mx(
+                out=turned[last][:].rearrange("p t m -> p (t m)"),
+                lhsT=x_words[g][:, last * CHUNK :].bitcast(FP8X4),
+                lhsT_scale=x_scales[g][:, last * CHUNK :],
+                rhs=w_words[g][:].bitcast(FP8X4),
+                rhs_scale=w_scales[g][:],
+                start=(g == 0),
+                stop=(g == PASSES - 1),
+            )
 
         own = []
         for c in range(CHUNKS):
             scaled = sbuf([P, PACK, P], F32, "scaled%d" % c, "scaled%d" % c)
             nc.scalar.activation(scaled[:], turned[c][:], COPY, scale=lam_cols[:, c : c + 1])
-            back = psum.tile([P, PACK, CHUNK], F32, name="back%d" % c, tag="bank%d" % [3, 2, 0, 1][c])
+            back = psum.tile([P, PACK, CHUNK], F32, name="back%d" % c, tag="bank%d" % [3, 2, 0, 7][c])
             for t in range(PACK):
                 nc.tensor.transpose(back[:, t, :], scaled[:, t, :], ident[:])
             own.append(back[:])
@@ -242,7 +247,7 @@ def tile_picked_mixup_none_e_kernel(
             parts = [[0], [1]] if c == CHUNKS - 1 else [[0, 1]]
             for halves in parts:
                 first = halves[0]
-                bank = "bank3" if first > 0 else "bank%d" % (4 + c)
+                bank = "bank3" if first > 0 else "bank%d" % [4, 5, 6, 1][c]
                 out_ps = psum.tile([P, len(halves), CHUNK], F32, name="out_ps%d_%d" % (c, first), tag=bank)
                 for half in halves:
                     nc.tensor.matmul_mx(

@@ -172,7 +172,7 @@ def tile_picked_mixup_none_e_kernel(
         h_tiles = []
         for t in range(PACK):
             h_sb = sbuf([P, S], F32, "h_sb%d" % t)
-            parts = [(0, HALF, "bank0"), (HALF, S, "bank1")] if t == 0 else [(0, S, ["", "bank2", "bank0", "bank1"][t])]
+            parts = [(0, HALF, "bank0"), (HALF, S, "bank1")] if t == 0 else [(0, S, ["", "bank2", "bank3", "bank0"][t])]
             for c0, c1, bank in parts:
                 h_ps = psum.tile([P, c1 - c0], F32, name="h_ps%d_%d" % (t, c0), tag=bank)
                 for g in range(PASSES):
@@ -205,7 +205,7 @@ def tile_picked_mixup_none_e_kernel(
             for c in range(CHUNKS - 1):
                 nc.tensor.transpose(turned[c][:, t, :], h_sb[:, c * CHUNK : (c + 1) * CHUNK], ident[:])
         last = CHUNKS - 1
-        turned[last] = psum.tile([P, PACK, P], F32, name="turned_last", tag="bank1")
+        turned[last] = psum.tile([P, PACK, P], F32, name="turned_last", tag="bank0")
         for g in range(PASSES):
             nc.tensor.matmul_mx(
                 out=turned[last][:].rearrange("p t m -> p (t m)"),
@@ -221,7 +221,7 @@ def tile_picked_mixup_none_e_kernel(
         for c in range(CHUNKS):
             scaled = sbuf([P, PACK, P], F32, "scaled%d" % c, "scaled%d" % c)
             nc.scalar.activation(scaled[:], turned[c][:], COPY, scale=lam_cols[:, c : c + 1])
-            back = psum.tile([P, PACK, CHUNK], F32, name="back%d" % c, tag="bank%d" % [3, 2, 0, 7][c])
+            back = psum.tile([P, PACK, CHUNK], F32, name="back%d" % c, tag="bank%d" % [1, 2, 3, 7][c])
             for t in range(PACK):
                 nc.tensor.transpose(back[:, t, :], scaled[:, t, :], ident[:])
             own.append(back[:])
@@ -247,7 +247,7 @@ def tile_picked_mixup_none_e_kernel(
             parts = [[0], [1]] if c == CHUNKS - 1 else [[0, 1]]
             for halves in parts:
                 first = halves[0]
-                bank = "bank3" if first > 0 else "bank%d" % [4, 5, 6, 1][c]
+                bank = "bank1" if first > 0 else "bank%d" % [4, 5, 6, 0][c]
                 out_ps = psum.tile([P, len(halves), CHUNK], F32, name="out_ps%d_%d" % (c, first), tag=bank)
                 for half in halves:
                     nc.tensor.matmul_mx(

@@ -31,9 +31,10 @@ GATHER = S // 2
 CHUNK = P
 CHUNKS = S // CHUNK
 HALF = S // 2
-X_WEAVE_VECTOR = 344
+X_WEAVE_VECTOR = [416, 336]
 W_FIRST_VECTOR = 32
 SCALAR_TILE = PACK - 1
+SPARE = 8
 
 
 def tile_picked_mixup_none_e_kernel(
@@ -95,39 +96,32 @@ def tile_picked_mixup_none_e_kernel(
 
         x_words = [sbuf([P, S], U32, "x_words%d" % g) for g in range(PASSES)]
         x_scales = [sbuf([P, S], U8, "x_scales%d" % g) for g in range(PASSES)]
+        def gather(engine, dst, window, lo, hi):
+            looked_up = window[:].indirect(entries(offs_sb, lo, hi))
+            if engine == "vector":
+                nc.vector.tensor_copy(dst, looked_up)
+            else:
+                nc.scalar.activation(dst, looked_up, COPY)
+
+        def weave(engine, dst, src):
+            dst = dst.rearrange("p (c r) j -> p c j r", r=RUN)
+            src = src.rearrange("p j (c r) -> p c j r", r=RUN)
+            if engine == "vector":
+                nc.vector.tensor_copy(out=dst, in_=src)
+            else:
+                nc.scalar.activation(dst, src, COPY)
+
         for g in range(PASSES):
             grouped = [sbuf([P, HALF, PACK], BF16, "x_grouped%d_%d" % (g, h)) for h in range(2)]
-            if g == 0:
-                planes = sbuf([P, PACK, S], BF16, "planes")
-            for u in range(2):
-                if g == 0:
-                    picked = planes[:, 2 * u : 2 * u + 2, :]
-                else:
-                    picked = sbuf([P, 2, S], BF16, "picked%d_%d" % (g, u))
-                for e in range(2):
-                    raw = x_raw[(g, 2 * u + e)]
-                    cut = 0 if e == 0 else HALF
-                    if cut > 0:
-                        nc.vector.tensor_copy(picked[:, e, :cut], raw[:].indirect(entries(offs_sb, 0, cut)))
-                    if cut < S:
-                        nc.scalar.activation(picked[:, e, cut:], raw[:].indirect(entries(offs_sb, cut, S)), COPY)
-                if g == 0:
-                    continue
-                cut = S if u == 0 else X_WEAVE_VECTOR
-                for h in range(2):
-                    lo = h * HALF
-                    dst = grouped[h][:, :, 2 * u : 2 * u + 2].rearrange("p (c r) e -> p c e r", r=RUN)
-                    src = picked[:, :, lo : lo + HALF].rearrange("p e (c r) -> p c e r", r=RUN)
-                    runs = min(max(cut - lo, 0), HALF) // RUN
-                    if runs > 0:
-                        nc.vector.tensor_copy(out=dst[:, :runs], in_=src[:, :runs])
-                    if runs < HALF // RUN:
-                        nc.scalar.activation(dst[:, runs:], src[:, runs:], COPY)
-            if g == 0:
-                for h in range(2):
-                    dst = grouped[h][:].rearrange("p (c r) j -> p c j r", r=RUN)
-                    src = planes[:, :, h * HALF : (h + 1) * HALF].rearrange("p j (c r) -> p c j r", r=RUN)
-                    nc.vector.tensor_copy(out=dst, in_=src)
+            planes = sbuf([P, PACK, S], BF16, "planes%d" % g)
+            gather("scalar", planes[:, 0, :], x_raw[(g, 0)], 0, S)
+            for j in range(1, PACK):
+                gather("vector", planes[:, j, :HALF], x_raw[(g, j)], 0, HALF)
+                gather("scalar", planes[:, j, HALF:], x_raw[(g, j)], HALF, S)
+            cut = X_WEAVE_VECTOR[g]
+            weave("vector", grouped[0][:], planes[:, :, :HALF])
+            weave("vector", grouped[1][:, : cut - HALF], planes[:, :, HALF:cut])
+            weave("scalar", grouped[1][:, cut - HALF :], planes[:, :, cut:])
             for h in range(2):
                 cols = slice(h * HALF, (h + 1) * HALF)
                 quantise(x_words[g][:, cols], x_scales[g][:, cols], grouped[h][:].rearrange("p c j -> p (c j)"))
@@ -138,7 +132,7 @@ def tile_picked_mixup_none_e_kernel(
             dealt = sbuf([P, 2, P, PACK], BF16, "w_dealt0_%d" % pair)
             src = w_first[:].rearrange("p j (m t) -> p m j t", t=PACK)[:, :, :, 2 * pair : 2 * pair + 2]
             dst = dealt[:].rearrange("p t m j -> p m j t")
-            cut = P if pair == 0 else 24
+            cut = 72 if pair == 0 else 48
             nc.vector.tensor_copy(out=dst[:, :cut], in_=src[:, :cut])
             if cut < P:
                 nc.scalar.activation(dst[:, cut:], src[:, cut:], COPY)
@@ -158,20 +152,35 @@ def tile_picked_mixup_none_e_kernel(
 
         deal("vector", 0, slice(0, 2), slice(0, P))
         deal("scalar", 0, slice(2, 4), slice(0, P))
-        deal("vector", 1, slice(0, 1), slice(0, 72))
-        deal("scalar", 1, slice(0, 1), slice(72, P))
-        deal("vector", 1, slice(2, 4), slice(0, 48))
+        deal("vector", 1, slice(0, 1), slice(0, P))
+        deal("vector", 1, slice(2, 4), slice(0, 32))
         deal("scalar", 1, slice(1, 2), slice(0, P))
-        deal("scalar", 1, slice(2, 4), slice(48, P))
+        deal("scalar", 1, slice(2, 4), slice(88, P))
         for t0, t1 in ((0, 1), (1, 2), (2, 4)):
+            if t0 == 1:
+                deal("vector", 1, slice(2, 4), slice(32, 88))
             cols = slice(t0 * P, t1 * P)
             flat = dealt[t0 // 2][:].rearrange("p t m j -> p (t m j)")
             quantise(w_words[1][:, cols], w_scales[1][:, cols], flat[:, t0 % 2 * K_PASS : (t0 % 2 + t1 - t0) * K_PASS])
 
         partner = sbuf([P, PACK, S], F32, "partner")
         h_tiles = []
+
+        def looked_up(t, c0):
+            return h_tiles[t][:].indirect(entries(pos_sb, c0, c0 + GATHER))
+
+        def times_mu(t, c0, values):
+            nc.vector.tensor_tensor(partner[:, t, c0 : c0 + GATHER], values, mu_sb[:, c0 : c0 + GATHER], MULT)
+
+        def fetch_on_scalar(c0):
+            fetched = sbuf([P, GATHER], F32, "fetched%d" % c0)
+            nc.scalar.activation(fetched[:], looked_up(SCALAR_TILE, c0), COPY)
+            times_mu(SCALAR_TILE, c0, fetched[:])
+
         for t in range(PACK):
-            h_sb = sbuf([P, S], F32, "h_sb%d" % t)
+            h_sb = sbuf([P, S + SPARE * (t != SCALAR_TILE)], F32, "h_sb%d" % t)
+            if t != SCALAR_TILE:
+                nc.gpsimd.memset(h_sb[:, S:], 0.0)
             parts = [(0, HALF, "bank0"), (HALF, S, "bank1")] if t == 0 else [(0, S, ["", "bank2", "bank3", "bank0"][t])]
             for c0, c1, bank in parts:
                 h_ps = psum.tile([P, c1 - c0], F32, name="h_ps%d_%d" % (t, c0), tag=bank)
@@ -189,42 +198,36 @@ def tile_picked_mixup_none_e_kernel(
                     nc.vector.tensor_copy(h_sb[:, c0:c1], h_ps[:])
                 else:
                     nc.scalar.activation(h_sb[:, c0:c1], h_ps[:], COPY)
-            if t == SCALAR_TILE:
-                fetched = sbuf([P, S], F32, "fetched")
-            for c0 in range(0, S, GATHER):
-                cols = slice(c0, c0 + GATHER)
-                looked_up = h_sb[:].indirect(entries(pos_sb, c0, c0 + GATHER))
-                if t == SCALAR_TILE:
-                    nc.scalar.activation(fetched[:, cols], looked_up, COPY)
-                    nc.vector.tensor_tensor(partner[:, t, cols], fetched[:, cols], mu_sb[:, cols], MULT)
-                else:
-                    nc.vector.tensor_tensor(partner[:, t, cols], looked_up, mu_sb[:, cols], MULT)
             h_tiles.append(h_sb)
-        turned = {c: psum.tile([P, PACK, P], F32, name="turned%d" % c, tag="bank%d" % (4 + c)) for c in range(CHUNKS - 1)}
-        for t, h_sb in enumerate(h_tiles):
-            for c in range(CHUNKS - 1):
-                nc.tensor.transpose(turned[c][:, t, :], h_sb[:, c * CHUNK : (c + 1) * CHUNK], ident[:])
-        last = CHUNKS - 1
-        turned[last] = psum.tile([P, PACK, P], F32, name="turned_last", tag="bank0")
+            if t < SCALAR_TILE:
+                nc.vector.tensor_tensor(partner[:, t, :], h_sb[:].indirect(pos_sb[:]), mu_sb[:], MULT)
+            else:
+                fetch_on_scalar(0)
+        turned = {c: psum.tile([P, PACK, P], F32, name="turned%d" % c, tag="bank%d" % [2, 4, 5, 6][c]) for c in range(CHUNKS)}
         for g in range(PASSES):
             nc.tensor.matmul_mx(
-                out=turned[last][:].rearrange("p t m -> p (t m)"),
-                lhsT=x_words[g][:, last * CHUNK :].bitcast(FP8X4),
-                lhsT_scale=x_scales[g][:, last * CHUNK :],
+                out=turned[0][:].rearrange("p t m -> p (t m)"),
+                lhsT=x_words[g][:, :CHUNK].bitcast(FP8X4),
+                lhsT_scale=x_scales[g][:, :CHUNK],
                 rhs=w_words[g][:].bitcast(FP8X4),
                 rhs_scale=w_scales[g][:],
                 start=(g == 0),
                 stop=(g == PASSES - 1),
             )
+        for t, h_sb in enumerate(h_tiles):
+            for c in range(1, CHUNKS):
+                nc.tensor.transpose(turned[c][:, t, :], h_sb[:, c * CHUNK : (c + 1) * CHUNK], ident[:])
 
         own = []
         for c in range(CHUNKS):
             scaled = sbuf([P, PACK, P], F32, "scaled%d" % c, "scaled%d" % c)
             nc.scalar.activation(scaled[:], turned[c][:], COPY, scale=lam_cols[:, c : c + 1])
-            back = psum.tile([P, PACK, CHUNK], F32, name="back%d" % c, tag="bank%d" % [1, 2, 3, 7][c])
+            back = psum.tile([P, PACK, CHUNK], F32, name="back%d" % c, tag="bank%d" % [1, 3, 0, 7][c])
             for t in range(PACK):
                 nc.tensor.transpose(back[:, t, :], scaled[:, t, :], ident[:])
             own.append(back[:])
+            if c == 0:
+                fetch_on_scalar(GATHER)
 
         out_view = out.rearrange("(half p) s -> p half s", p=P)
         for c in range(CHUNKS):
@@ -236,7 +239,7 @@ def tile_picked_mixup_none_e_kernel(
                 partner[:, :, cols].rearrange("p t (c r) -> p c t r", r=RUN),
                 ADD,
             )
-            z_words = sbuf([P, CHUNK], U32, "z_words%d" % c, "scaled%d" % (c + 2) if c + 2 < CHUNKS else "")
+            z_words = sbuf([P, CHUNK], U32, "z_words%d" % c)
             z_scales = sbuf([P, CHUNK], U8, "z_scales%d" % c)
             nc.vector.quantize_mx(
                 out=z_words[:].bitcast(FP8X4),
@@ -247,7 +250,7 @@ def tile_picked_mixup_none_e_kernel(
             parts = [[0], [1]] if c == CHUNKS - 1 else [[0, 1]]
             for halves in parts:
                 first = halves[0]
-                bank = "bank1" if first > 0 else "bank%d" % [4, 5, 6, 0][c]
+                bank = "bank1" if first > 0 else "bank%d" % [2, 4, 5, 6][c]
                 out_ps = psum.tile([P, len(halves), CHUNK], F32, name="out_ps%d_%d" % (c, first), tag=bank)
                 for half in halves:
                     nc.tensor.matmul_mx(

@@ -26,15 +26,19 @@ QUADRANT = 32
 SCALE_ROWS = 4
 LIST_ROWS = 16
 RUN = 4
-
-GATHER = S // 2
+HALF = S // 2
 CHUNK = P
 CHUNKS = S // CHUNK
-HALF = S // 2
-X_WEAVE_VECTOR = [416, 336]
-W_FIRST_VECTOR = 32
-SCALAR_TILE = PACK - 1
-SPARE = 8
+LAST_TILE = PACK - 1
+
+WEAVE_VECTOR = [416, 336]
+FIRST_PASS_VECTOR = [72, 48]
+LAST_ROWS_VECTOR = [32, 88]
+
+H_BANKS = [[0, 1], [2], [3], [0]]
+TURNED_BANKS = [2, 4, 5, 6]
+BACK_BANKS = [1, 3, 0, 7]
+SPLIT_OUT_BANK = BACK_BANKS[0]
 
 
 def tile_picked_mixup_none_e_kernel(
@@ -45,18 +49,30 @@ def tile_picked_mixup_none_e_kernel(
         keep = ctx.enter_context(tc.tile_pool(name="keep", bufs=1))
         psum = ctx.enter_context(tc.psum_pool(name="psum", bufs=1))
 
-        def sbuf(shape, dtype, name, tag=""):
-            return keep.tile(shape, dtype, name=name, tag=tag, align_bytes=64)
+        def sbuf(shape, dtype, name):
+            return keep.tile(shape, dtype, name=name, align_bytes=64)
+
+        def bank(shape, name, number):
+            return psum.tile(shape, F32, name=name, tag="bank%d" % number)
 
         def entries(offsets, lo, hi):
             return offsets[:, lo // LIST_ROWS : hi // LIST_ROWS]
+
+        def on_vector(dst, src):
+            nc.vector.tensor_copy(out=dst, in_=src)
+
+        def on_scalar(dst, src):
+            nc.scalar.activation(dst, src, COPY)
+
+        def quantise(words, scales, grouped):
+            nc.vector.quantize_mx(out=words.bitcast(FP8X4), scales=scales, in_=grouped)
 
         w2_scale_sb = sbuf([P, N], U8, "w2_scale_sb")
         nc.gpsimd.memset(w2_scale_sb[:], 0)
         ident = sbuf([P, P], F32, "ident")
         zeros = sbuf([P, P], F32, "zeros")
         nc.vector.memset(zeros[:], 0.0)
-        nc.scalar.activation(ident[:], zeros[:], COPY)
+        on_scalar(ident[:], zeros[:])
         make_identity(nc, ident[:], nomemset=True)
 
         offs_sb = sbuf([P, S // LIST_ROWS], U16, "offs_sb")
@@ -64,11 +80,11 @@ def tile_picked_mixup_none_e_kernel(
         w_rows = w1.rearrange("(g p j) c -> g p j c", g=PASSES, j=PACK)
         x_rows = xT.rearrange("(g p j) c -> g p j c", g=PASSES, j=PACK)
         w_first = sbuf([P, PACK, H], F32, "w_first")
-        x_raw = {}
+        x_plane = {}
         for g in range(PASSES):
             for j in range(PACK):
-                x_raw[(g, j)] = sbuf([P, T], F32, "x_raw%d_%d" % (g, j))
-                nc.sync.dma_start(out=x_raw[(g, j)][:], in_=x_rows[g, :, j, :])
+                x_plane[(g, j)] = sbuf([P, T], F32, "x_plane%d_%d" % (g, j))
+                nc.sync.dma_start(out=x_plane[(g, j)][:], in_=x_rows[g, :, j, :])
                 if (g, j) == (0, 0):
                     nc.sync.dma_start(offs_sb[:], offs)
         nc.sync.dma_start(out=w_first[:], in_=w_rows[0])
@@ -91,119 +107,101 @@ def tile_picked_mixup_none_e_kernel(
                 in_=w2_scales[0, SCALE_ROWS * q : SCALE_ROWS * (q + 1), :].bitcast(I32),
             )
 
-        def quantise(words, scales, grouped):
-            nc.vector.quantize_mx(out=words.bitcast(FP8X4), scales=scales, in_=grouped)
-
         x_words = [sbuf([P, S], U32, "x_words%d" % g) for g in range(PASSES)]
         x_scales = [sbuf([P, S], U8, "x_scales%d" % g) for g in range(PASSES)]
-        def gather(engine, dst, window, lo, hi):
-            looked_up = window[:].indirect(entries(offs_sb, lo, hi))
-            if engine == "vector":
-                nc.vector.tensor_copy(dst, looked_up)
-            else:
-                nc.scalar.activation(dst, looked_up, COPY)
 
-        def weave(engine, dst, src):
-            dst = dst.rearrange("p (c r) j -> p c j r", r=RUN)
-            src = src.rearrange("p j (c r) -> p c j r", r=RUN)
-            if engine == "vector":
-                nc.vector.tensor_copy(out=dst, in_=src)
-            else:
-                nc.scalar.activation(dst, src, COPY)
+        def weave(move, dst, src):
+            move(dst.rearrange("p (c r) j -> p c j r", r=RUN), src.rearrange("p j (c r) -> p c j r", r=RUN))
 
         for g in range(PASSES):
             grouped = [sbuf([P, HALF, PACK], BF16, "x_grouped%d_%d" % (g, h)) for h in range(2)]
-            planes = sbuf([P, PACK, S], BF16, "planes%d" % g)
-            gather("scalar", planes[:, 0, :], x_raw[(g, 0)], 0, S)
+            picked = sbuf([P, PACK, S], BF16, "picked%d" % g)
+            on_scalar(picked[:, 0, :], x_plane[(g, 0)][:].indirect(offs_sb[:]))
             for j in range(1, PACK):
-                gather("vector", planes[:, j, :HALF], x_raw[(g, j)], 0, HALF)
-                gather("scalar", planes[:, j, HALF:], x_raw[(g, j)], HALF, S)
-            cut = X_WEAVE_VECTOR[g]
-            weave("vector", grouped[0][:], planes[:, :, :HALF])
-            weave("vector", grouped[1][:, : cut - HALF], planes[:, :, HALF:cut])
-            weave("scalar", grouped[1][:, cut - HALF :], planes[:, :, cut:])
+                on_vector(picked[:, j, :HALF], x_plane[(g, j)][:].indirect(entries(offs_sb, 0, HALF)))
+                on_scalar(picked[:, j, HALF:], x_plane[(g, j)][:].indirect(entries(offs_sb, HALF, S)))
+            cut = WEAVE_VECTOR[g]
+            weave(on_vector, grouped[0][:], picked[:, :, :HALF])
+            weave(on_vector, grouped[1][:, : cut - HALF], picked[:, :, HALF:cut])
+            weave(on_scalar, grouped[1][:, cut - HALF :], picked[:, :, cut:])
             for h in range(2):
                 cols = slice(h * HALF, (h + 1) * HALF)
                 quantise(x_words[g][:, cols], x_scales[g][:, cols], grouped[h][:].rearrange("p c j -> p (c j)"))
 
         w_words = [sbuf([P, H], U32, "w_words%d" % g) for g in range(PASSES)]
         w_scales = [sbuf([P, H], U8, "w_scales%d" % g) for g in range(PASSES)]
-        for pair in range(2):
-            dealt = sbuf([P, 2, P, PACK], BF16, "w_dealt0_%d" % pair)
+        for pair, cut in enumerate(FIRST_PASS_VECTOR):
+            first_dealt = sbuf([P, 2, P, PACK], BF16, "first_dealt%d" % pair)
             src = w_first[:].rearrange("p j (m t) -> p m j t", t=PACK)[:, :, :, 2 * pair : 2 * pair + 2]
-            dst = dealt[:].rearrange("p t m j -> p m j t")
-            cut = 72 if pair == 0 else 48
-            nc.vector.tensor_copy(out=dst[:, :cut], in_=src[:, :cut])
-            if cut < P:
-                nc.scalar.activation(dst[:, cut:], src[:, cut:], COPY)
+            dst = first_dealt[:].rearrange("p t m j -> p m j t")
+            on_vector(dst[:, :cut], src[:, :cut])
+            on_scalar(dst[:, cut:], src[:, cut:])
             cols = slice(2 * P * pair, 2 * P * (pair + 1))
-            quantise(w_words[0][:, cols], w_scales[0][:, cols], dealt[:].rearrange("p t m j -> p (t m j)"))
+            quantise(w_words[0][:, cols], w_scales[0][:, cols], first_dealt[:].rearrange("p t m j -> p (t m j)"))
 
-        dealt = [sbuf([P, 2, P, PACK], BF16, "w_dealt1_%d" % pair) for pair in range(2)]
-        def deal(engine, u, tiles, cols):
-            pair = tiles.start // 2
-            src = w_last[u][:].rearrange("p e (m t) -> p m e t", t=PACK)[:, cols, :, tiles]
-            dst = dealt[pair][:, tiles.start % 2 : (tiles.stop - 1) % 2 + 1, cols, 2 * u : 2 * u + 2]
-            dst = dst.rearrange("p t m e -> p m e t")
-            if engine == "vector":
-                nc.vector.tensor_copy(out=dst, in_=src)
-            else:
-                nc.scalar.activation(dst, src, COPY)
+        last_dealt = [sbuf([P, 2, P, PACK], BF16, "last_dealt%d" % pair) for pair in range(2)]
 
-        deal("vector", 0, slice(0, 2), slice(0, P))
-        deal("scalar", 0, slice(2, 4), slice(0, P))
-        deal("vector", 1, slice(0, 1), slice(0, P))
-        deal("vector", 1, slice(2, 4), slice(0, 32))
-        deal("scalar", 1, slice(1, 2), slice(0, P))
-        deal("scalar", 1, slice(2, 4), slice(88, P))
-        for t0, t1 in ((0, 1), (1, 2), (2, 4)):
-            if t0 == 1:
-                deal("vector", 1, slice(2, 4), slice(32, 88))
+        def deal_last(move, u, t0, t1, m0, m1):
+            src = w_last[u][:].rearrange("p e (m t) -> p m e t", t=PACK)[:, m0:m1, :, t0:t1]
+            dst = last_dealt[t0 // 2][:, t0 % 2 : t0 % 2 + t1 - t0, m0:m1, 2 * u : 2 * u + 2]
+            move(dst.rearrange("p t m e -> p m e t"), src)
+
+        def quantise_last(t0, t1):
             cols = slice(t0 * P, t1 * P)
-            flat = dealt[t0 // 2][:].rearrange("p t m j -> p (t m j)")
+            flat = last_dealt[t0 // 2][:].rearrange("p t m j -> p (t m j)")
             quantise(w_words[1][:, cols], w_scales[1][:, cols], flat[:, t0 % 2 * K_PASS : (t0 % 2 + t1 - t0) * K_PASS])
+
+        before, after = LAST_ROWS_VECTOR
+        deal_last(on_vector, 0, 0, 2, 0, P)
+        deal_last(on_scalar, 0, 2, 4, 0, P)
+        deal_last(on_vector, 1, 0, 1, 0, P)
+        deal_last(on_vector, 1, 2, 4, 0, before)
+        deal_last(on_scalar, 1, 1, 2, 0, P)
+        deal_last(on_scalar, 1, 2, 4, after, P)
+        quantise_last(0, 1)
+        deal_last(on_vector, 1, 2, 4, before, after)
+        quantise_last(1, 2)
+        quantise_last(2, 4)
 
         partner = sbuf([P, PACK, S], F32, "partner")
         h_tiles = []
 
         def looked_up(t, c0):
-            return h_tiles[t][:].indirect(entries(pos_sb, c0, c0 + GATHER))
+            return h_tiles[t][:].indirect(entries(pos_sb, c0, c0 + HALF))
 
         def times_mu(t, c0, values):
-            nc.vector.tensor_tensor(partner[:, t, c0 : c0 + GATHER], values, mu_sb[:, c0 : c0 + GATHER], MULT)
+            nc.vector.tensor_tensor(partner[:, t, c0 : c0 + HALF], values, mu_sb[:, c0 : c0 + HALF], MULT)
 
         def fetch_on_scalar(c0):
-            fetched = sbuf([P, GATHER], F32, "fetched%d" % c0)
-            nc.scalar.activation(fetched[:], looked_up(SCALAR_TILE, c0), COPY)
-            times_mu(SCALAR_TILE, c0, fetched[:])
+            fetched = sbuf([P, HALF], F32, "fetched%d" % c0)
+            on_scalar(fetched[:], looked_up(LAST_TILE, c0))
+            times_mu(LAST_TILE, c0, fetched[:])
 
-        for t in range(PACK):
-            h_sb = sbuf([P, S + SPARE * (t != SCALAR_TILE)], F32, "h_sb%d" % t)
-            if t != SCALAR_TILE:
-                nc.gpsimd.memset(h_sb[:, S:], 0.0)
-            parts = [(0, HALF, "bank0"), (HALF, S, "bank1")] if t == 0 else [(0, S, ["", "bank2", "bank3", "bank0"][t])]
-            for c0, c1, bank in parts:
-                h_ps = psum.tile([P, c1 - c0], F32, name="h_ps%d_%d" % (t, c0), tag=bank)
+        for t, banks in enumerate(H_BANKS):
+            h_sb = sbuf([P, S], F32, "h_sb%d" % t)
+            width = S // len(banks)
+            for part, (number, move) in enumerate(zip(banks, (on_scalar, on_vector))):
+                cols = slice(part * width, (part + 1) * width)
+                h_ps = bank([P, width], "h_ps%d_%d" % (t, part), number)
                 for g in range(PASSES):
                     nc.tensor.matmul_mx(
                         out=h_ps[:],
                         lhsT=w_words[g][:, t * P : (t + 1) * P].bitcast(FP8X4),
                         lhsT_scale=w_scales[g][:, t * P : (t + 1) * P],
-                        rhs=x_words[g][:, c0:c1].bitcast(FP8X4),
-                        rhs_scale=x_scales[g][:, c0:c1],
+                        rhs=x_words[g][:, cols].bitcast(FP8X4),
+                        rhs_scale=x_scales[g][:, cols],
                         start=(g == 0),
                         stop=(g == PASSES - 1),
                     )
-                if (t, c0) == (0, HALF):
-                    nc.vector.tensor_copy(h_sb[:, c0:c1], h_ps[:])
-                else:
-                    nc.scalar.activation(h_sb[:, c0:c1], h_ps[:], COPY)
+                move(h_sb[:, cols], h_ps[:])
             h_tiles.append(h_sb)
-            if t < SCALAR_TILE:
-                nc.vector.tensor_tensor(partner[:, t, :], h_sb[:].indirect(pos_sb[:]), mu_sb[:], MULT)
-            else:
+            if t == LAST_TILE:
                 fetch_on_scalar(0)
-        turned = {c: psum.tile([P, PACK, P], F32, name="turned%d" % c, tag="bank%d" % [2, 4, 5, 6][c]) for c in range(CHUNKS)}
+            else:
+                for c0 in range(0, S, HALF):
+                    times_mu(t, c0, looked_up(t, c0))
+
+        turned = [bank([P, PACK, P], "turned%d" % c, TURNED_BANKS[c]) for c in range(CHUNKS)]
         for g in range(PASSES):
             nc.tensor.matmul_mx(
                 out=turned[0][:].rearrange("p t m -> p (t m)"),
@@ -220,50 +218,44 @@ def tile_picked_mixup_none_e_kernel(
 
         own = []
         for c in range(CHUNKS):
-            scaled = sbuf([P, PACK, P], F32, "scaled%d" % c, "scaled%d" % c)
+            scaled = sbuf([P, PACK, P], F32, "scaled%d" % c)
             nc.scalar.activation(scaled[:], turned[c][:], COPY, scale=lam_cols[:, c : c + 1])
-            back = psum.tile([P, PACK, CHUNK], F32, name="back%d" % c, tag="bank%d" % [1, 3, 0, 7][c])
+            back = bank([P, PACK, CHUNK], "back%d" % c, BACK_BANKS[c])
             for t in range(PACK):
                 nc.tensor.transpose(back[:, t, :], scaled[:, t, :], ident[:])
-            own.append(back[:])
+            own.append(back)
             if c == 0:
-                fetch_on_scalar(GATHER)
+                fetch_on_scalar(HALF)
 
-        out_view = out.rearrange("(half p) s -> p half s", p=P)
+        out_view = out.rearrange("(b p) s -> p b s", p=P)
         for c in range(CHUNKS):
             cols = slice(c * CHUNK, (c + 1) * CHUNK)
             z_grouped = sbuf([P, CHUNK, PACK], BF16, "z_grouped%d" % c)
             nc.vector.tensor_tensor(
                 z_grouped[:].rearrange("p (c r) t -> p c t r", r=RUN),
-                own[c].rearrange("p t (c r) -> p c t r", r=RUN),
+                own[c][:].rearrange("p t (c r) -> p c t r", r=RUN),
                 partner[:, :, cols].rearrange("p t (c r) -> p c t r", r=RUN),
                 ADD,
             )
             z_words = sbuf([P, CHUNK], U32, "z_words%d" % c)
             z_scales = sbuf([P, CHUNK], U8, "z_scales%d" % c)
-            nc.vector.quantize_mx(
-                out=z_words[:].bitcast(FP8X4),
-                scales=z_scales[:],
-                in_=z_grouped[:].rearrange("p c t -> p (c t)"),
-            )
+            quantise(z_words[:], z_scales[:], z_grouped[:].rearrange("p c t -> p (c t)"))
             out_sb = sbuf([P, N // P, CHUNK], F32, "out_sb%d" % c)
-            parts = [[0], [1]] if c == CHUNKS - 1 else [[0, 1]]
-            for halves in parts:
-                first = halves[0]
-                bank = "bank1" if first > 0 else "bank%d" % [2, 4, 5, 6][c]
-                out_ps = psum.tile([P, len(halves), CHUNK], F32, name="out_ps%d_%d" % (c, first), tag=bank)
-                for half in halves:
+            if c == CHUNKS - 1:
+                groups = [(0, 1, TURNED_BANKS[c], on_scalar), (1, 2, SPLIT_OUT_BANK, on_vector)]
+            else:
+                groups = [(0, 2, TURNED_BANKS[c], on_scalar)]
+            for b0, b1, number, move in groups:
+                out_ps = bank([P, b1 - b0, CHUNK], "out_ps%d_%d" % (c, b0), number)
+                for b in range(b0, b1):
                     nc.tensor.matmul_mx(
-                        out=out_ps[:, half - first, :],
-                        lhsT=w2_sb[:, 2 * P * half : 2 * P * (half + 1)].bitcast(FP4X4),
-                        lhsT_scale=w2_scale_sb[:, P * half : P * (half + 1)],
+                        out=out_ps[:, b - b0, :],
+                        lhsT=w2_sb[:, 2 * P * b : 2 * P * (b + 1)].bitcast(FP4X4),
+                        lhsT_scale=w2_scale_sb[:, P * b : P * (b + 1)],
                         rhs=z_words[:].bitcast(FP8X4),
                         rhs_scale=z_scales[:],
                         start=True,
                         stop=True,
                     )
-                if first > 0:
-                    nc.vector.tensor_copy(out_sb[:, first:, :], out_ps[:])
-                else:
-                    nc.scalar.activation(out_sb[:, : len(halves), :], out_ps[:], COPY)
+                move(out_sb[:, b0:b1, :], out_ps[:])
             nc.sync.dma_start(out=out_view[:, :, cols], in_=out_sb[:])

@@ -17,6 +17,8 @@ FP4X4 = mybir.dt.float4_e2m1fn_x4
 COPY = mybir.ActivationFunctionType.Copy
 MULT = mybir.AluOpType.mult
 ADD = mybir.AluOpType.add
+MAX = mybir.AluOpType.max
+IS_LT = mybir.AluOpType.is_lt
 
 P = 128
 PACK = 4
@@ -30,15 +32,19 @@ HALF = S // 2
 CHUNK = P
 CHUNKS = S // CHUNK
 LAST_TILE = PACK - 1
+SUMMED = (0, 1)
+BLOCK = 32
+TINY = 2.0**-60
 
 WEAVE_VECTOR = [416, 336]
 FIRST_PASS_VECTOR = [72, 48]
 LAST_ROWS_VECTOR = [32, 88]
 
 H_BANKS = [[0, 1], [2], [3], [0]]
-TURNED_BANKS = [2, 4, 5, 6]
-BACK_BANKS = [1, 3, 0, 7]
-SPLIT_OUT_BANK = BACK_BANKS[0]
+FACTOR_BANK = 7
+TURNED_BANKS = [4, 5, 3, 3]
+BACK_BANKS = [7, 2, 1, 0]
+OUT_BANKS = [[6], [4], [5], [0, 1]]
 
 
 def tile_picked_mixup_none_e_kernel(
@@ -49,8 +55,8 @@ def tile_picked_mixup_none_e_kernel(
         keep = ctx.enter_context(tc.tile_pool(name="keep", bufs=1))
         psum = ctx.enter_context(tc.psum_pool(name="psum", bufs=1))
 
-        def sbuf(shape, dtype, name):
-            return keep.tile(shape, dtype, name=name, align_bytes=64)
+        def sbuf(shape, dtype, name, tag=None):
+            return keep.tile(shape, dtype, name=name, tag=tag or name, align_bytes=64)
 
         def bank(shape, name, number):
             return psum.tile(shape, F32, name=name, tag="bank%d" % number)
@@ -80,6 +86,8 @@ def tile_picked_mixup_none_e_kernel(
         w_rows = w1.rearrange("(g p j) c -> g p j c", g=PASSES, j=PACK)
         x_rows = xT.rearrange("(g p j) c -> g p j c", g=PASSES, j=PACK)
         w_first = sbuf([P, PACK, H], F32, "w_first")
+        share_rows = sbuf([P, 2 * P], F32, "share_rows")
+        nc.vector.memset(share_rows[:], 0.0)
         x_plane = {}
         for g in range(PASSES):
             for j in range(PACK):
@@ -87,6 +95,11 @@ def tile_picked_mixup_none_e_kernel(
                 nc.sync.dma_start(out=x_plane[(g, j)][:], in_=x_rows[g, :, j, :])
                 if (g, j) == (0, 0):
                     nc.sync.dma_start(offs_sb[:], offs)
+                    for v, share in enumerate((lam, mu)):
+                        nc.sync.dma_start(
+                            out=share_rows[0:P:BLOCK, v * P : (v + 1) * P].rearrange("q (c i) -> q c i", i=BLOCK),
+                            in_=share[0].rearrange("(c q i) -> q c i", c=CHUNKS, i=BLOCK),
+                        )
         nc.sync.dma_start(out=w_first[:], in_=w_rows[0])
         w_last = []
         for u in range(2):
@@ -94,11 +107,6 @@ def tile_picked_mixup_none_e_kernel(
             nc.sync.dma_start(out=raw[:], in_=w_rows[1, :, 2 * u : 2 * u + 2, :])
             w_last.append(raw)
         nc.sync.dma_start(pos_sb[:], pos1)
-        mu_sb = sbuf([P, S], F32, "mu_sb")
-        nc.sync.dma_start(out=mu_sb[:], in_=mu)
-        lam_cols = sbuf([P, CHUNKS], F32, "lam_cols")
-        with nc.allow_non_contiguous_dma(reason="one value a partition"):
-            nc.sync.dma_start(out=lam_cols[:], in_=lam[0].rearrange("(c p) -> p c", p=P))
         w2_sb = sbuf([P, 2 * N], U8, "w2_sb")
         nc.sync.dma_start(out=w2_sb[:], in_=w2_words[0])
         for q in range(P // QUADRANT):
@@ -106,6 +114,24 @@ def tile_picked_mixup_none_e_kernel(
                 out=w2_scale_sb[QUADRANT * q : QUADRANT * q + SCALE_ROWS, :].bitcast(I32),
                 in_=w2_scales[0, SCALE_ROWS * q : SCALE_ROWS * (q + 1), :].bitcast(I32),
             )
+
+        share_cols = sbuf([P, 2 * P], F32, "share_cols")
+        nc.vector.transpose(share_cols[:], share_rows[:])
+        lam_cols = share_cols[:, 0:P:BLOCK]
+        mu_cols = share_cols[:, P : 2 * P : BLOCK]
+        lam_sum = lam_cols[:, : len(SUMMED)]
+        small = [sbuf([P, len(SUMMED)], F32, "small%d" % i) for i in range(5)]
+        size, raise_by, safe_lam, inverse, quotient = small
+        nc.vector.scalar_tensor_tensor(size[:], lam_sum, -1.0, lam_sum, MULT, MAX)
+        nc.vector.tensor_scalar(raise_by[:], size[:], TINY, TINY, IS_LT, MULT)
+        nc.vector.tensor_tensor(safe_lam[:], raise_by[:], lam_sum, ADD)
+        nc.vector.reciprocal(inverse[:], safe_lam[:])
+        nc.vector.tensor_tensor(quotient[:], inverse[:], mu_cols[:, : len(SUMMED)], MULT)
+        factor_ps = bank([P, CHUNKS, CHUNK], "factor_ps", FACTOR_BANK)
+        for c in range(CHUNKS):
+            column = quotient[:, c : c + 1] if c in SUMMED else mu_cols[:, c : c + 1]
+            nc.tensor.transpose(factor_ps[:, c, :], column.to_broadcast([P, P]), ident[:])
+        factor = sbuf([P, S], F32, "factor")
 
         x_words = [sbuf([P, S], U32, "x_words%d" % g) for g in range(PASSES)]
         x_scales = [sbuf([P, S], U8, "x_scales%d" % g) for g in range(PASSES)]
@@ -120,6 +146,8 @@ def tile_picked_mixup_none_e_kernel(
             for j in range(1, PACK):
                 on_vector(picked[:, j, :HALF], x_plane[(g, j)][:].indirect(entries(offs_sb, 0, HALF)))
                 on_scalar(picked[:, j, HALF:], x_plane[(g, j)][:].indirect(entries(offs_sb, HALF, S)))
+            if g == 0:
+                on_scalar(factor[:], factor_ps[:].rearrange("p c s -> p (c s)"))
             cut = WEAVE_VECTOR[g]
             weave(on_vector, grouped[0][:], picked[:, :, :HALF])
             weave(on_vector, grouped[1][:, : cut - HALF], picked[:, :, HALF:cut])
@@ -163,24 +191,20 @@ def tile_picked_mixup_none_e_kernel(
         quantise_last(1, 2)
         quantise_last(2, 4)
 
-        partner = sbuf([P, PACK, S], F32, "partner")
         h_tiles = []
 
-        def looked_up(t, c0):
-            return h_tiles[t][:].indirect(entries(pos_sb, c0, c0 + HALF))
+        def looked_up(t, lo, hi):
+            return h_tiles[t][:].indirect(entries(pos_sb, lo, hi))
 
-        def times_mu(t, c0, values):
-            nc.vector.tensor_tensor(partner[:, t, c0 : c0 + HALF], values, mu_sb[:, c0 : c0 + HALF], MULT)
+        partner = [sbuf([P, PACK, HALF], F32, "partner0")]
 
-        def fetch_on_scalar(c0):
-            fetched = sbuf([P, HALF], F32, "fetched%d" % c0)
-            on_scalar(fetched[:], looked_up(LAST_TILE, c0))
-            times_mu(LAST_TILE, c0, fetched[:])
+        def times_factor(t, half, values):
+            nc.vector.tensor_tensor(partner[half][:, t, :], values, factor[:, half * HALF : (half + 1) * HALF], MULT)
 
         for t, banks in enumerate(H_BANKS):
             h_sb = sbuf([P, S], F32, "h_sb%d" % t)
             width = S // len(banks)
-            for part, (number, move) in enumerate(zip(banks, (on_scalar, on_vector))):
+            for part, (number, move) in enumerate(zip(banks, (on_vector, on_scalar) if len(banks) == 2 else (on_scalar,))):
                 cols = slice(part * width, (part + 1) * width)
                 h_ps = bank([P, width], "h_ps%d_%d" % (t, part), number)
                 for g in range(PASSES):
@@ -195,67 +219,126 @@ def tile_picked_mixup_none_e_kernel(
                     )
                 move(h_sb[:, cols], h_ps[:])
             h_tiles.append(h_sb)
-            if t == LAST_TILE:
-                fetch_on_scalar(0)
-            else:
-                for c0 in range(0, S, HALF):
-                    times_mu(t, c0, looked_up(t, c0))
+            times_factor(t, 0, looked_up(t, 0, HALF))
 
-        turned = [bank([P, PACK, P], "turned%d" % c, TURNED_BANKS[c]) for c in range(CHUNKS)]
+        turned = {c: bank([P, PACK, P], "turned%d" % c, TURNED_BANKS[c]) for c in SUMMED}
+
+        def turn_into_sums(t, term, start, stop):
+            for c in SUMMED:
+                cols = slice(c * CHUNK, (c + 1) * CHUNK)
+                nc.tensor.matmul(turned[c][:, t, :], term[:, cols], ident[:], start=start, stop=stop, is_transpose=True)
+
+        own = {}
+
+        def scale_own(c):
+            scaled = sbuf([P, PACK, P], F32, "scaled%d" % c)
+            nc.scalar.activation(scaled[:], turned[c][:], COPY, scale=lam_cols[:, c : c + 1])
+            own[c] = bank([P, PACK, CHUNK], "back%d" % c, BACK_BANKS[c])
+            for t in range(PACK):
+                nc.tensor.transpose(own[c][:, t, :], scaled[:, t, :], ident[:])
+
+        turn_into_sums(0, h_tiles[0], True, False)
+        turn_into_sums(0, partner[0][:, 0, :], False, False)
+        turn_into_sums(1, h_tiles[1], False, False)
+        turned[2] = bank([P, PACK, P], "turned2", TURNED_BANKS[2])
         for g in range(PASSES):
             nc.tensor.matmul_mx(
-                out=turned[0][:].rearrange("p t m -> p (t m)"),
-                lhsT=x_words[g][:, :CHUNK].bitcast(FP8X4),
-                lhsT_scale=x_scales[g][:, :CHUNK],
+                out=turned[2][:].rearrange("p t m -> p (t m)"),
+                lhsT=x_words[g][:, 2 * CHUNK : 3 * CHUNK].bitcast(FP8X4),
+                lhsT_scale=x_scales[g][:, 2 * CHUNK : 3 * CHUNK],
                 rhs=w_words[g][:].bitcast(FP8X4),
                 rhs_scale=w_scales[g][:],
                 start=(g == 0),
                 stop=(g == PASSES - 1),
             )
+        turn_into_sums(1, partner[0][:, 1, :], False, False)
+        turn_into_sums(2, h_tiles[2], False, False)
+        turn_into_sums(LAST_TILE, h_tiles[LAST_TILE], False, False)
+        turn_into_sums(2, partner[0][:, 2, :], False, False)
+        turn_into_sums(LAST_TILE, partner[0][:, LAST_TILE, :], False, True)
+        fetched = sbuf([P, HALF], F32, "fetched")
+        on_scalar(fetched[:], looked_up(LAST_TILE, HALF, S))
+        scale_own(2)
+        turned[3] = bank([P, PACK, P], "turned3", TURNED_BANKS[3])
         for t, h_sb in enumerate(h_tiles):
-            for c in range(1, CHUNKS):
-                nc.tensor.transpose(turned[c][:, t, :], h_sb[:, c * CHUNK : (c + 1) * CHUNK], ident[:])
-
-        own = []
-        for c in range(CHUNKS):
-            scaled = sbuf([P, PACK, P], F32, "scaled%d" % c)
-            nc.scalar.activation(scaled[:], turned[c][:], COPY, scale=lam_cols[:, c : c + 1])
-            back = bank([P, PACK, CHUNK], "back%d" % c, BACK_BANKS[c])
-            for t in range(PACK):
-                nc.tensor.transpose(back[:, t, :], scaled[:, t, :], ident[:])
-            own.append(back)
-            if c == 0:
-                fetch_on_scalar(HALF)
-
-        out_view = out.rearrange("(b p) s -> p b s", p=P)
-        for c in range(CHUNKS):
-            cols = slice(c * CHUNK, (c + 1) * CHUNK)
-            z_grouped = sbuf([P, CHUNK, PACK], BF16, "z_grouped%d" % c)
+            nc.tensor.transpose(turned[3][:, t, :], h_sb[:, 3 * CHUNK :], ident[:])
+        partner.append(sbuf([P, PACK, HALF], F32, "partner1", tag="x_words1"))
+        times_factor(0, 1, looked_up(0, HALF, S))
+        times_factor(LAST_TILE, 1, fetched[:])
+        times_factor(1, 1, looked_up(1, HALF, S))
+        for lo in range(HALF, S, CHUNK):
             nc.vector.tensor_tensor(
-                z_grouped[:].rearrange("p (c r) t -> p c t r", r=RUN),
+                partner[1][:, 2, lo - HALF : lo - HALF + CHUNK], looked_up(2, lo, lo + CHUNK), factor[:, lo : lo + CHUNK], MULT
+            )
+
+        z_grouped = {}
+        for c in SUMMED:
+            z_turned = sbuf([P, 2, P, 2], BF16, "z_turned%d" % c)
+            nc.scalar.activation(
+                z_turned[:], turned[c][:].rearrange("p (u e) m -> p u m e", e=2), COPY, scale=safe_lam[:, c : c + 1]
+            )
+            own[c] = bank([P, 2, CHUNK], "pairs%d" % c, BACK_BANKS[c])
+            for u in range(2):
+                nc.tensor.transpose(own[c][:, u, :], z_turned[:, u].rearrange("p m e -> p (m e)").bitcast(F32), ident[:])
+
+        def unload(c):
+            z_grouped[c] = sbuf([P, CHUNK, PACK], BF16, "z_grouped%d" % c)
+            nc.scalar.copy(
+                z_grouped[c][:].rearrange("p s t -> p (s t)").bitcast(F32).rearrange("p (s u) -> p s u", u=2),
+                own[c][:].rearrange("p u s -> p s u"),
+            )
+
+        def add_terms(c, place):
+            z_grouped[c] = sbuf([P, CHUNK, PACK], BF16, "z_grouped%d" % c, tag=place)
+            nc.vector.tensor_tensor(
+                z_grouped[c][:].rearrange("p (c r) t -> p c t r", r=RUN),
                 own[c][:].rearrange("p t (c r) -> p c t r", r=RUN),
-                partner[:, :, cols].rearrange("p t (c r) -> p c t r", r=RUN),
+                partner[1][:, :, (c - 2) * CHUNK : (c - 1) * CHUNK].rearrange("p t (c r) -> p c t r", r=RUN),
                 ADD,
             )
-            z_words = sbuf([P, CHUNK], U32, "z_words%d" % c)
+
+        out_view = out.rearrange("(b p) s -> p b s", p=P)
+        z_words = {}
+        results = {}
+
+        def multiply(c):
+            z_words[c] = sbuf([P, CHUNK], U32, "z_words%d" % c, tag="z_grouped0" if c == 2 else None)
             z_scales = sbuf([P, CHUNK], U8, "z_scales%d" % c)
-            quantise(z_words[:], z_scales[:], z_grouped[:].rearrange("p c t -> p (c t)"))
-            out_sb = sbuf([P, N // P, CHUNK], F32, "out_sb%d" % c)
-            if c == CHUNKS - 1:
-                groups = [(0, 1, TURNED_BANKS[c], on_scalar), (1, 2, SPLIT_OUT_BANK, on_vector)]
-            else:
-                groups = [(0, 2, TURNED_BANKS[c], on_scalar)]
-            for b0, b1, number, move in groups:
-                out_ps = bank([P, b1 - b0, CHUNK], "out_ps%d_%d" % (c, b0), number)
-                for b in range(b0, b1):
+            quantise(z_words[c][:], z_scales[:], z_grouped[c][:].rearrange("p c t -> p (c t)"))
+            blocks = N // P // len(OUT_BANKS[c])
+            results[c] = []
+            for part, number in enumerate(OUT_BANKS[c]):
+                out_ps = bank([P, blocks, CHUNK], "out_ps%d_%d" % (c, part), number)
+                for i in range(blocks):
+                    b = part * blocks + i
                     nc.tensor.matmul_mx(
-                        out=out_ps[:, b - b0, :],
+                        out=out_ps[:, i, :],
                         lhsT=w2_sb[:, 2 * P * b : 2 * P * (b + 1)].bitcast(FP4X4),
                         lhsT_scale=w2_scale_sb[:, P * b : P * (b + 1)],
-                        rhs=z_words[:].bitcast(FP8X4),
+                        rhs=z_words[c][:].bitcast(FP8X4),
                         rhs_scale=z_scales[:],
                         start=True,
                         stop=True,
                     )
-                move(out_sb[:, b0:b1, :], out_ps[:])
-            nc.sync.dma_start(out=out_view[:, :, cols], in_=out_sb[:])
+                results[c].append(out_ps)
+
+        def store(c, moves):
+            out_sb = sbuf([P, N // P, CHUNK], F32, "out_sb%d" % c)
+            blocks = N // P // len(moves)
+            for part, move in enumerate(moves):
+                move(out_sb[:, part * blocks : (part + 1) * blocks, :], results[c][part][:])
+            nc.sync.dma_start(out=out_view[:, :, c * CHUNK : (c + 1) * CHUNK], in_=out_sb[:])
+
+        scale_own(3)
+        unload(0)
+        unload(1)
+        add_terms(2, None)
+        multiply(0)
+        store(0, [on_scalar])
+        multiply(1)
+        store(1, [on_scalar])
+        multiply(2)
+        store(2, [on_scalar])
+        add_terms(3, "z_grouped1")
+        multiply(3)
+        store(3, [on_vector, on_scalar])

@@ -156,6 +156,17 @@ def tile_picked_mixup_none_e_kernel(
                 cols = slice(h * HALF, (h + 1) * HALF)
                 quantise(x_words[g][:, cols], x_scales[g][:, cols], grouped[h][:].rearrange("p c j -> p (c j)"))
 
+        warm = bank([P, HALF], "warm", 6)
+        nc.tensor.matmul_mx(
+            out=warm[:],
+            lhsT=x_words[1][:, HALF : HALF + P].bitcast(FP8X4),
+            lhsT_scale=x_scales[1][:, HALF : HALF + P],
+            rhs=x_words[1][:, HALF:].bitcast(FP8X4),
+            rhs_scale=x_scales[1][:, HALF:],
+            start=True,
+            stop=True,
+        )
+
         w_words = [sbuf([P, H], U32, "w_words%d" % g) for g in range(PASSES)]
         w_scales = [sbuf([P, H], U8, "w_scales%d" % g) for g in range(PASSES)]
         for pair, cut in enumerate(FIRST_PASS_VECTOR):

@@ -232,12 +232,15 @@ def tile_picked_mixup_none_e_kernel(
             h_tiles.append(h_sb)
             times_factor(t, 0, looked_up(t, 0, HALF))
 
-        turned = {c: bank([P, PACK, P], "turned%d" % c, TURNED_BANKS[c]) for c in SUMMED}
+        sums = [bank([P, len(SUMMED), 2, P], "sums%d" % u, TURNED_BANKS[u]) for u in range(2)]
+        turned = {}
 
         def turn_into_sums(t, term, start, stop):
             for c in SUMMED:
                 cols = slice(c * CHUNK, (c + 1) * CHUNK)
-                nc.tensor.matmul(turned[c][:, t, :], term[:, cols], ident[:], start=start, stop=stop, is_transpose=True)
+                nc.tensor.matmul(
+                    sums[t // 2][:, c, t % 2, :], term[:, cols], ident[:], start=start and c == 0, stop=stop and c == 1, is_transpose=True
+                )
 
         own = {}
 
@@ -262,35 +265,36 @@ def tile_picked_mixup_none_e_kernel(
                 start=(g == 0),
                 stop=(g == PASSES - 1),
             )
-        turn_into_sums(1, partner[0][:, 1, :], False, False)
-        turn_into_sums(2, h_tiles[2], False, False)
+        turn_into_sums(1, partner[0][:, 1, :], False, True)
+        turn_into_sums(2, h_tiles[2], True, False)
         turn_into_sums(LAST_TILE, h_tiles[LAST_TILE], False, False)
         turn_into_sums(2, partner[0][:, 2, :], False, False)
         turn_into_sums(LAST_TILE, partner[0][:, LAST_TILE, :], False, True)
         fetched = sbuf([P, HALF], F32, "fetched")
-        on_scalar(fetched[:], looked_up(LAST_TILE, HALF, S))
+        on_scalar(fetched[:], looked_up(2, HALF, S))
         scale_own(2)
         turned[3] = bank([P, PACK, P], "turned3", TURNED_BANKS[3])
         for t, h_sb in enumerate(h_tiles):
             nc.tensor.transpose(turned[3][:, t, :], h_sb[:, 3 * CHUNK :], ident[:])
         partner.append(sbuf([P, PACK, HALF], F32, "partner1", tag="x_words1"))
         times_factor(0, 1, looked_up(0, HALF, S))
-        times_factor(LAST_TILE, 1, fetched[:])
+        times_factor(2, 1, fetched[:])
         times_factor(1, 1, looked_up(1, HALF, S))
         for lo in range(HALF, S, CHUNK):
             nc.vector.tensor_tensor(
-                partner[1][:, 2, lo - HALF : lo - HALF + CHUNK], looked_up(2, lo, lo + CHUNK), factor[:, lo : lo + CHUNK], MULT
+                partner[1][:, LAST_TILE, lo - HALF : lo - HALF + CHUNK], looked_up(LAST_TILE, lo, lo + CHUNK), factor[:, lo : lo + CHUNK], MULT
             )
 
         z_grouped = {}
+        z_turned = [sbuf([P, 2, P, 2], BF16, "z_turned%d" % c) for c in SUMMED]
         for c in SUMMED:
-            z_turned = sbuf([P, 2, P, 2], BF16, "z_turned%d" % c)
-            nc.scalar.activation(
-                z_turned[:], turned[c][:].rearrange("p (u e) m -> p u m e", e=2), COPY, scale=safe_lam[:, c : c + 1]
-            )
             own[c] = bank([P, 2, CHUNK], "pairs%d" % c, BACK_BANKS[c])
-            for u in range(2):
-                nc.tensor.transpose(own[c][:, u, :], z_turned[:, u].rearrange("p m e -> p (m e)").bitcast(F32), ident[:])
+        for u in range(2):
+            for c in SUMMED:
+                nc.scalar.activation(
+                    z_turned[c][:, u], sums[u][:, c].rearrange("p e m -> p m e"), COPY, scale=safe_lam[:, c : c + 1]
+                )
+                nc.tensor.transpose(own[c][:, u, :], z_turned[c][:, u].rearrange("p m e -> p (m e)").bitcast(F32), ident[:])
 
         def unload(c):
             z_grouped[c] = sbuf([P, CHUNK, PACK], BF16, "z_grouped%d" % c)

from contextlib import ExitStack

import concourse.mybir as mybir
from concourse.masks import make_identity

K, T, S, H, N = 1024, 1024, 512, 512, 256
FLOPS = 2 * K * H * S + 2 * H * N * S

F32 = mybir.dt.float32
BF16 = mybir.dt.bfloat16
I32 = mybir.dt.int32
U32 = mybir.dt.uint32
U16 = mybir.dt.uint16
U8 = mybir.dt.uint8
FP8X4 = mybir.dt.float8_e4m3fn_x4
FP4X4 = mybir.dt.float4_e2m1fn_x4
COPY = mybir.ActivationFunctionType.Copy
MULT = mybir.AluOpType.mult
ADD = mybir.AluOpType.add
MAX = mybir.AluOpType.max
IS_LT = mybir.AluOpType.is_lt

P = 128
PACK = 4
K_PASS = P * PACK
PASSES = K // K_PASS
QUADRANT = 32
SCALE_ROWS = 4
LIST_ROWS = 16
RUN = 4
HALF = S // 2
CHUNK = P
CHUNKS = S // CHUNK
LAST_TILE = PACK - 1
SUMMED = (0, 1)
BLOCK = 32
TINY = 2.0**-60

WEAVE_VECTOR = [416, 336]
FIRST_PASS_VECTOR = [72, 48]
LAST_ROWS_VECTOR = [32, 88]

H_BANKS = [[0, 1], [2], [3], [0]]
FACTOR_BANK = 7
TURNED_BANKS = [4, 5, 3, 3]
BACK_BANKS = [7, 2, 1, 0]
OUT_BANKS = [[6], [4], [5], [0, 1]]


def tile_picked_mixup_none_e_kernel(
    tc, xT, w1, w2_words, w2_scales, lam, mu, offs, pos1, out
):
    nc = tc.nc
    with ExitStack() as ctx:
        keep = ctx.enter_context(tc.tile_pool(name="keep", bufs=1))
        psum = ctx.enter_context(tc.psum_pool(name="psum", bufs=1))

        def sbuf(shape, dtype, name, tag=None):
            return keep.tile(shape, dtype, name=name, tag=tag or name, align_bytes=64)

        def bank(shape, name, number):
            return psum.tile(shape, F32, name=name, tag="bank%d" % number)

        def entries(offsets, lo, hi):
            return offsets[:, lo // LIST_ROWS : hi // LIST_ROWS]

        def on_vector(dst, src):
            nc.vector.tensor_copy(out=dst, in_=src)

        def on_scalar(dst, src):
            nc.scalar.activation(dst, src, COPY)

        def quantise(words, scales, grouped):
            nc.vector.quantize_mx(out=words.bitcast(FP8X4), scales=scales, in_=grouped)

        w2_scale_sb = sbuf([P, N], U8, "w2_scale_sb")
        nc.gpsimd.memset(w2_scale_sb[:], 0)
        ident = sbuf([P, P], F32, "ident")
        zeros = sbuf([P, P], F32, "zeros")
        nc.vector.memset(zeros[:], 0.0)
        on_scalar(ident[:], zeros[:])
        make_identity(nc, ident[:], nomemset=True)

        offs_sb = sbuf([P, S // LIST_ROWS], U16, "offs_sb")
        pos_sb = sbuf([P, S // LIST_ROWS], U16, "pos_sb")
        w_rows = w1.rearrange("(g p j) c -> g p j c", g=PASSES, j=PACK)
        x_rows = xT.rearrange("(g p j) c -> g p j c", g=PASSES, j=PACK)
        w_first = sbuf([P, PACK, H], F32, "w_first")
        share_rows = sbuf([P, 2 * P], F32, "share_rows")
        nc.vector.memset(share_rows[:], 0.0)
        x_plane = {}
        for g in range(PASSES):
            for j in range(PACK):
                x_plane[(g, j)] = sbuf([P, T], F32, "x_plane%d_%d" % (g, j))
                nc.sync.dma_start(out=x_plane[(g, j)][:], in_=x_rows[g, :, j, :])
                if (g, j) == (0, 0):
                    nc.sync.dma_start(offs_sb[:], offs)
                    for v, share in enumerate((lam, mu)):
                        nc.sync.dma_start(
                            out=share_rows[0:P:BLOCK, v * P : (v + 1) * P].rearrange("q (c i) -> q c i", i=BLOCK),
                            in_=share[0].rearrange("(c q i) -> q c i", c=CHUNKS, i=BLOCK),
                        )
        nc.sync.dma_start(out=w_first[:], in_=w_rows[0])
        w_last = []
        for u in range(2):
            raw = sbuf([P, 2, H], F32, "w_last%d" % u)
            nc.sync.dma_start(out=raw[:], in_=w_rows[1, :, 2 * u : 2 * u + 2, :])
            w_last.append(raw)
        nc.sync.dma_start(pos_sb[:], pos1)
        w2_sb = sbuf([P, 2 * N], U8, "w2_sb")
        nc.sync.dma_start(out=w2_sb[:], in_=w2_words[0])
        for q in range(P // QUADRANT):
            nc.sync.dma_start(
                out=w2_scale_sb[QUADRANT * q : QUADRANT * q + SCALE_ROWS, :].bitcast(I32),
                in_=w2_scales[0, SCALE_ROWS * q : SCALE_ROWS * (q + 1), :].bitcast(I32),
            )

        share_cols = sbuf([P, 2 * P], F32, "share_cols")
        nc.vector.transpose(share_cols[:], share_rows[:])
        lam_cols = share_cols[:, 0:P:BLOCK]
        mu_cols = share_cols[:, P : 2 * P : BLOCK]
        lam_sum = lam_cols[:, : len(SUMMED)]
        small = [sbuf([P, len(SUMMED)], F32, "small%d" % i) for i in range(5)]
        size, raise_by, safe_lam, inverse, quotient = small
        nc.vector.scalar_tensor_tensor(size[:], lam_sum, -1.0, lam_sum, MULT, MAX)
        nc.vector.tensor_scalar(raise_by[:], size[:], TINY, TINY, IS_LT, MULT)
        nc.vector.tensor_tensor(safe_lam[:], raise_by[:], lam_sum, ADD)
        nc.vector.reciprocal(inverse[:], safe_lam[:])
        nc.vector.tensor_tensor(quotient[:], inverse[:], mu_cols[:, : len(SUMMED)], MULT)
        factor_ps = bank([P, CHUNKS, CHUNK], "factor_ps", FACTOR_BANK)
        for c in range(CHUNKS):
            column = quotient[:, c : c + 1] if c in SUMMED else mu_cols[:, c : c + 1]
            nc.tensor.transpose(factor_ps[:, c, :], column.to_broadcast([P, P]), ident[:])
        factor = sbuf([P, S], F32, "factor")

        x_words = [sbuf([P, S], U32, "x_words%d" % g) for g in range(PASSES)]
        x_scales = [sbuf([P, S], U8, "x_scales%d" % g) for g in range(PASSES)]

        def weave(move, dst, src):
            move(dst.rearrange("p (c r) j -> p c j r", r=RUN), src.rearrange("p j (c r) -> p c j r", r=RUN))

        for g in range(PASSES):
            grouped = [sbuf([P, HALF, PACK], BF16, "x_grouped%d_%d" % (g, h)) for h in range(2)]
            picked = sbuf([P, PACK, S], BF16, "picked%d" % g)
            on_scalar(picked[:, 0, :], x_plane[(g, 0)][:].indirect(offs_sb[:]))
            for j in range(1, PACK):
                on_vector(picked[:, j, :HALF], x_plane[(g, j)][:].indirect(entries(offs_sb, 0, HALF)))
                on_scalar(picked[:, j, HALF:], x_plane[(g, j)][:].indirect(entries(offs_sb, HALF, S)))
            if g == 0:
                on_scalar(factor[:], factor_ps[:].rearrange("p c s -> p (c s)"))
            cut = WEAVE_VECTOR[g]
            weave(on_vector, grouped[0][:], picked[:, :, :HALF])
            weave(on_vector, grouped[1][:, : cut - HALF], picked[:, :, HALF:cut])
            weave(on_scalar, grouped[1][:, cut - HALF :], picked[:, :, cut:])
            for h in range(2):
                cols = slice(h * HALF, (h + 1) * HALF)
                quantise(x_words[g][:, cols], x_scales[g][:, cols], grouped[h][:].rearrange("p c j -> p (c j)"))

        warm = bank([P, HALF], "warm", 6)
        nc.tensor.matmul_mx(
            out=warm[:],
            lhsT=x_words[1][:, HALF : HALF + P].bitcast(FP8X4),
            lhsT_scale=x_scales[1][:, HALF : HALF + P],
            rhs=x_words[1][:, HALF:].bitcast(FP8X4),
            rhs_scale=x_scales[1][:, HALF:],
            start=True,
            stop=True,
        )

        w_words = [sbuf([P, H], U32, "w_words%d" % g) for g in range(PASSES)]
        w_scales = [sbuf([P, H], U8, "w_scales%d" % g) for g in range(PASSES)]
        for pair, cut in enumerate(FIRST_PASS_VECTOR):
            first_dealt = sbuf([P, 2, P, PACK], BF16, "first_dealt%d" % pair)
            src = w_first[:].rearrange("p j (m t) -> p m j t", t=PACK)[:, :, :, 2 * pair : 2 * pair + 2]
            dst = first_dealt[:].rearrange("p t m j -> p m j t")
            on_vector(dst[:, :cut], src[:, :cut])
            on_scalar(dst[:, cut:], src[:, cut:])
            cols = slice(2 * P * pair, 2 * P * (pair + 1))
            quantise(w_words[0][:, cols], w_scales[0][:, cols], first_dealt[:].rearrange("p t m j -> p (t m j)"))

        last_dealt = [sbuf([P, 2, P, PACK], BF16, "last_dealt%d" % pair) for pair in range(2)]

        def deal_last(move, u, t0, t1, m0, m1):
            src = w_last[u][:].rearrange("p e (m t) -> p m e t", t=PACK)[:, m0:m1, :, t0:t1]
            dst = last_dealt[t0 // 2][:, t0 % 2 : t0 % 2 + t1 - t0, m0:m1, 2 * u : 2 * u + 2]
            move(dst.rearrange("p t m e -> p m e t"), src)

        def quantise_last(t0, t1):
            cols = slice(t0 * P, t1 * P)
            flat = last_dealt[t0 // 2][:].rearrange("p t m j -> p (t m j)")
            quantise(w_words[1][:, cols], w_scales[1][:, cols], flat[:, t0 % 2 * K_PASS : (t0 % 2 + t1 - t0) * K_PASS])

        before, after = LAST_ROWS_VECTOR
        deal_last(on_vector, 0, 0, 2, 0, P)
        deal_last(on_scalar, 0, 2, 4, 0, P)
        deal_last(on_vector, 1, 0, 1, 0, P)
        deal_last(on_vector, 1, 2, 4, 0, before)
        deal_last(on_scalar, 1, 1, 2, 0, P)
        deal_last(on_scalar, 1, 2, 4, after, P)
        quantise_last(0, 1)
        deal_last(on_vector, 1, 2, 4, before, after)
        quantise_last(1, 2)
        quantise_last(2, 4)

        h_tiles = []

        def looked_up(t, lo, hi):
            return h_tiles[t][:].indirect(entries(pos_sb, lo, hi))

        partner = [sbuf([P, PACK, HALF], F32, "partner0")]

        def times_factor(t, half, values):
            nc.vector.tensor_tensor(partner[half][:, t, :], values, factor[:, half * HALF : (half + 1) * HALF], MULT)

        for t, banks in enumerate(H_BANKS):
            h_sb = sbuf([P, S], F32, "h_sb%d" % t)
            width = S // len(banks)
            for part, (number, move) in enumerate(zip(banks, (on_vector, on_scalar) if len(banks) == 2 else (on_scalar,))):
                cols = slice(part * width, (part + 1) * width)
                h_ps = bank([P, width], "h_ps%d_%d" % (t, part), number)
                for g in range(PASSES):
                    nc.tensor.matmul_mx(
                        out=h_ps[:],
                        lhsT=w_words[g][:, t * P : (t + 1) * P].bitcast(FP8X4),
                        lhsT_scale=w_scales[g][:, t * P : (t + 1) * P],
                        rhs=x_words[g][:, cols].bitcast(FP8X4),
                        rhs_scale=x_scales[g][:, cols],
                        start=(g == 0),
                        stop=(g == PASSES - 1),
                    )
                move(h_sb[:, cols], h_ps[:])
            h_tiles.append(h_sb)
            times_factor(t, 0, looked_up(t, 0, HALF))

        sums = [bank([P, len(SUMMED), 2, P], "sums%d" % u, TURNED_BANKS[u]) for u in range(2)]
        turned = {}

        def turn_into_sums(t, term, start, stop):
            for c in SUMMED:
                cols = slice(c * CHUNK, (c + 1) * CHUNK)
                nc.tensor.matmul(
                    sums[t // 2][:, c, t % 2, :], term[:, cols], ident[:], start=start and c == 0, stop=stop and c == 1, is_transpose=True
                )

        own = {}

        def scale_own(c):
            scaled = sbuf([P, PACK, P], F32, "scaled%d" % c)
            nc.scalar.activation(scaled[:], turned[c][:], COPY, scale=lam_cols[:, c : c + 1])
            own[c] = bank([P, PACK, CHUNK], "back%d" % c, BACK_BANKS[c])
            for t in range(PACK):
                nc.tensor.transpose(own[c][:, t, :], scaled[:, t, :], ident[:])

        turn_into_sums(0, h_tiles[0], True, False)
        turn_into_sums(0, partner[0][:, 0, :], False, False)
        turn_into_sums(1, h_tiles[1], False, False)
        turned[2] = bank([P, PACK, P], "turned2", TURNED_BANKS[2])
        for g in range(PASSES):
            nc.tensor.matmul_mx(
                out=turned[2][:].rearrange("p t m -> p (t m)"),
                lhsT=x_words[g][:, 2 * CHUNK : 3 * CHUNK].bitcast(FP8X4),
                lhsT_scale=x_scales[g][:, 2 * CHUNK : 3 * CHUNK],
                rhs=w_words[g][:].bitcast(FP8X4),
                rhs_scale=w_scales[g][:],
                start=(g == 0),
                stop=(g == PASSES - 1),
            )
        turn_into_sums(1, partner[0][:, 1, :], False, True)
        turn_into_sums(2, h_tiles[2], True, False)
        turn_into_sums(LAST_TILE, h_tiles[LAST_TILE], False, False)
        turn_into_sums(2, partner[0][:, 2, :], False, False)
        turn_into_sums(LAST_TILE, partner[0][:, LAST_TILE, :], False, True)
        fetched = sbuf([P, HALF], F32, "fetched")
        on_scalar(fetched[:], looked_up(2, HALF, S))
        scale_own(2)
        turned[3] = bank([P, PACK, P], "turned3", TURNED_BANKS[3])
        for t, h_sb in enumerate(h_tiles):
            nc.tensor.transpose(turned[3][:, t, :], h_sb[:, 3 * CHUNK :], ident[:])
        partner.append(sbuf([P, PACK, HALF], F32, "partner1", tag="x_words1"))
        times_factor(0, 1, looked_up(0, HALF, S))
        times_factor(2, 1, fetched[:])
        times_factor(1, 1, looked_up(1, HALF, S))
        for lo in range(HALF, S, CHUNK):
            nc.vector.tensor_tensor(
                partner[1][:, LAST_TILE, lo - HALF : lo - HALF + CHUNK], looked_up(LAST_TILE, lo, lo + CHUNK), factor[:, lo : lo + CHUNK], MULT
            )

        z_grouped = {}
        z_turned = [sbuf([P, 2, P, 2], BF16, "z_turned%d" % c) for c in SUMMED]
        for c in SUMMED:
            own[c] = bank([P, 2, CHUNK], "pairs%d" % c, BACK_BANKS[c])
        for u in range(2):
            for c in SUMMED:
                nc.scalar.activation(
                    z_turned[c][:, u], sums[u][:, c].rearrange("p e m -> p m e"), COPY, scale=safe_lam[:, c : c + 1]
                )
                nc.tensor.transpose(own[c][:, u, :], z_turned[c][:, u].rearrange("p m e -> p (m e)").bitcast(F32), ident[:])

        def unload(c):
            z_grouped[c] = sbuf([P, CHUNK, PACK], BF16, "z_grouped%d" % c)
            nc.scalar.copy(
                z_grouped[c][:].rearrange("p s t -> p (s t)").bitcast(F32).rearrange("p (s u) -> p s u", u=2),
                own[c][:].rearrange("p u s -> p s u"),
            )

        def add_terms(c, place):
            z_grouped[c] = sbuf([P, CHUNK, PACK], BF16, "z_grouped%d" % c, tag=place)
            nc.vector.tensor_tensor(
                z_grouped[c][:].rearrange("p (c r) t -> p c t r", r=RUN),
                own[c][:].rearrange("p t (c r) -> p c t r", r=RUN),
                partner[1][:, :, (c - 2) * CHUNK : (c - 1) * CHUNK].rearrange("p t (c r) -> p c t r", r=RUN),
                ADD,
            )

        out_view = out.rearrange("(b p) s -> p b s", p=P)
        z_words = {}
        results = {}

        def multiply(c):
            z_words[c] = sbuf([P, CHUNK], U32, "z_words%d" % c, tag="z_grouped0" if c == 2 else None)
            z_scales = sbuf([P, CHUNK], U8, "z_scales%d" % c)
            quantise(z_words[c][:], z_scales[:], z_grouped[c][:].rearrange("p c t -> p (c t)"))
            blocks = N // P // len(OUT_BANKS[c])
            results[c] = []
            for part, number in enumerate(OUT_BANKS[c]):
                out_ps = bank([P, blocks, CHUNK], "out_ps%d_%d" % (c, part), number)
                for i in range(blocks):
                    b = part * blocks + i
                    nc.tensor.matmul_mx(
                        out=out_ps[:, i, :],
                        lhsT=w2_sb[:, 2 * P * b : 2 * P * (b + 1)].bitcast(FP4X4),
                        lhsT_scale=w2_scale_sb[:, P * b : P * (b + 1)],
                        rhs=z_words[c][:].bitcast(FP8X4),
                        rhs_scale=z_scales[:],
                        start=True,
                        stop=True,
                    )
                results[c].append(out_ps)

        def store(c, moves):
            out_sb = sbuf([P, N // P, CHUNK], F32, "out_sb%d" % c)
            blocks = N // P // len(moves)
            for part, move in enumerate(moves):
                move(out_sb[:, part * blocks : (part + 1) * blocks, :], results[c][part][:])
            nc.sync.dma_start(out=out_view[:, :, c * CHUNK : (c + 1) * CHUNK], in_=out_sb[:])

        scale_own(3)
        unload(0)
        unload(1)
        add_terms(2, None)
        multiply(0)
        store(0, [on_scalar])
        multiply(1)
        store(1, [on_scalar])
        multiply(2)
        store(2, [on_scalar])
        add_terms(3, "z_grouped1")
        multiply(3)
        store(3, [on_vector, on_scalar])
